import numpy as np
import ml_dtypes


def mxq(x, axis, fmt="e4m3"):
    dtype, down = {"e4m3": (ml_dtypes.float8_e4m3fn, 7), "e5m2": (ml_dtypes.float8_e5m2, 14)}[fmt]
    v = np.moveaxis(np.asarray(x, np.float32).astype(ml_dtypes.bfloat16).astype(np.float64), axis, -1)
    blocks = v.reshape(v.shape[:-1] + (-1, 32))
    amax = np.abs(blocks).max(-1, keepdims=True)
    byte = np.maximum(np.where(amax > 0, np.frexp(amax)[1] - 1 + 127, 0) - down, 1)
    scale = np.exp2(byte - 127.0)
    codes = (blocks / scale).astype(np.float32).astype(dtype).astype(np.float64)
    return np.moveaxis((codes * scale).reshape(v.shape), -1, axis)


WIDE = False


def mx_kscale(k):
    if not WIDE:
        return np.ones(k)
    levels = np.array([10, -10, 5, -5, 0])
    if k % 512:
        return np.exp2(np.random.permutation(np.resize(levels, k // 32))).repeat(32)
    a = np.empty((k // 512, 16))
    for p in range(k // 512):
        a[p, :8] = np.random.permutation(np.resize(levels, 8))
        for g in range(8):
            far = levels[np.abs(levels - a[p, g]) >= 10]
            a[p, g + 8] = far[np.random.randint(len(far))]
    return np.exp2(a.ravel()).repeat(32)


BF16 = ml_dtypes.bfloat16


def bf(x):
    return np.asarray(x, np.float32).astype(BF16)


def f64(x):
    return np.asarray(x).astype(np.float64)


B, D, X = 1024, 1024, 512


def _euler(state, z):
    return state + 0.5 * (np.tanh(z) - 0.5 * state)


def draw0():
    s, t = mx_kscale(X), mx_kscale(D)
    return {"h": bf(np.random.standard_normal((B, D)) * 0.5),
            "x": bf(np.random.standard_normal((B, X)) * s),
            "w": bf(np.random.standard_normal((D, D)) * np.sqrt(2.0 / D)),
            "win": bf(np.random.standard_normal((X, D)) / np.sqrt(X) / s[:, None]),
            "b": bf(np.random.standard_normal(D) * 0.3),
            "p": bf((1.0 + 0.25 * np.random.standard_normal(D)) * t),
            "r": bf((1.0 + 0.25 * np.random.standard_normal(D)) / t)}


def core(h, x, w, win, b, p, r):
    h, w, b, p, r = f64(h), f64(w), f64(b), f64(p), f64(r)
    a = mxq(r[:, None] * (w - w.T), 0, "e4m3")
    c = (mxq(f64(x), 1, "e4m3") @ mxq(f64(win), 0, "e4m3")) + b[None, :]
    z1 = (mxq(h * p[None, :], 1, "e4m3") @ a) + c
    u1 = _euler(h, z1)
    z2 = (mxq(u1 * p[None, :], 1, "e4m3") @ a) + c
    return 0.5 * h + 0.5 * _euler(u1, z2)


def e4m3fn_bytes(y):
    return np.clip(np.asarray(y, np.float64), -448.0, 448.0).astype(np.float32).astype(ml_dtypes.float8_e4m3fn).view(np.uint8)


def e4m3fn_values(b):
    return np.asarray(b, np.uint8).view(ml_dtypes.float8_e4m3fn).astype(np.float64)


def setup_inputs():
    d = draw0()
    x0 = np.asarray(d['x']).astype(np.float64)
    s = (np.max(np.abs(x0), axis=(0,), keepdims=True) / 448.0).astype(np.float32)
    out = {}
    for k, v in d.items():
        if k == 'x':
            out['x_bytes'] = e4m3fn_bytes(x0 / s.astype(np.float64))
            out['x_scale'] = s
        else:
            out[k] = v
    return out


def reference(h, x_bytes, x_scale, w, win, b, p, r):
    return core(h, e4m3fn_values(x_bytes) * x_scale.astype(np.float64), w, win, b, p, r)

@@ -1,0 +1,528 @@
+from contextlib import ExitStack
+
+import concourse.mybir as mybir
+from concourse.masks import make_identity
+
+F32 = mybir.dt.float32
+BF16 = mybir.dt.bfloat16
+U32 = mybir.dt.uint32
+U8 = mybir.dt.uint8
+FP8 = mybir.dt.float8_e4m3fn
+FP8X4 = mybir.dt.float8_e4m3fn_x4
+ALU = mybir.AluOpType
+ACT = mybir.ActivationFunctionType
+
+B, D, X = 1024, 1024, 512
+P = 128
+T = 4
+N = P * T
+G = D // N
+H = B // N
+ACC = ((0, 0), (0, 1), (1, 0),)
+FLOPS = 2 * B * D * (X + 2 * D)
+
+
+def tile_antisymmetricssprk2step_kernel(tc, h, x_bytes, x_scale, w, win, b, p, r, out):
+    nc = tc.nc
+    with ExitStack() as ctx:
+        keep = ctx.enter_context(tc.tile_pool(name="keep", bufs=1))
+        work = ctx.enter_context(tc.tile_pool(name="work", bufs=2))
+        psum = ctx.enter_context(tc.psum_pool(name="psum", bufs=4))
+        ctx.enter_context(tc.manual_schedule())
+
+        def kt(name, shape, dtype, align=64):
+            return keep.tile(shape, dtype, name=name, align_bytes=align)
+
+        def page(name, shape, dtype):
+            return work.tile(shape, dtype, name=name, tag="page", bufs=7, align_bytes=64)
+
+        def mix(name, shape):
+            return work.tile(shape, BF16, name=name, tag="mix", bufs=12, align_bytes=64)
+
+        def grid(name, shape, dtype, na, nb):
+            return {(i, j): kt("%s%d%d" % (name, i, j), shape, dtype) for i in range(na) for j in range(nb)}
+
+        r_col = kt("r_col", [P, G, T], BF16)
+        p_col = kt("p_col", [P, G, T], BF16)
+        b_col = kt("b_col", [P, G, T], BF16)
+        s_col = kt("s_col", [P, T], F32)
+        nc.scalar.dma_start(out=r_col[:], in_=r.rearrange("(g p t) -> p g t", p=P, t=T))
+        nc.scalar.dma_start(out=p_col[:], in_=p.rearrange("(g p t) -> p g t", p=P, t=T))
+        nc.gpsimd.dma_start(out=s_col[:], in_=x_scale.rearrange("o (p t) -> p (o t)", p=P, t=T))
+        nc.gpsimd.dma_start(out=b_col[:], in_=b.rearrange("(g p t) -> p g t", p=P, t=T))
+
+        w_rows = w.rearrange("(g p t) c -> g p t c", p=P, t=T)
+        h_rows = h.rearrange("(g p t) c -> g p t c", p=P, t=T)
+        x_rows = x_bytes.rearrange("(g p t) c -> g p t c", p=P, t=T)
+        out_rows = out.rearrange("(g p t) c -> g p t c", p=P, t=T)
+        w_nat = [page("w_nat%d" % g, [P, T, D], BF16) for g in range(G)]
+        h_nat = [kt("h_nat%d" % g, [P, T, D], BF16) for g in range(H)]
+        x_raw = [kt("x_raw%d" % g, [P, T, X], U8) for g in range(H)]
+        win_nat = page("win_nat", [P, T, D], BF16)
+        for t in range(T):
+            nc.sync.dma_start(out=w_nat[0][:, t:t + 1, :], in_=w_rows[0, :, t:t + 1, :])
+        nc.sync.dma_start(out=h_nat[0][:], in_=h_rows[0])
+        for t in range(0, T, 2):
+            nc.sync.dma_start(out=w_nat[1][:, t:t + 2, :], in_=w_rows[1, :, t:t + 2, :])
+        nc.sync.dma_start(out=x_raw[0][:], in_=x_rows[0])
+        nc.sync.dma_start(out=win_nat[:], in_=win.rearrange("(p t) c -> p t c", p=P, t=T))
+        nc.sync.dma_start(out=x_raw[1][:], in_=x_rows[1])
+        nc.sync.dma_start(out=h_nat[1][:], in_=h_rows[1])
+
+        ident = kt("ident", [P, P], F32)
+        ident_b = kt("ident_b", [P, P], BF16)
+        make_identity(nc, ident[:])
+        warm = kt("warm", [P, 1], F32)
+        nc.vector.memset(warm[:], 0.0)
+        nc.scalar.activation(warm[:], warm[:], ACT.Tanh)
+        dg = kt("dg", [P, G * T, P], BF16)
+        dn = kt("dn", [P, G * T, P], BF16)
+        nc.vector.tensor_copy(ident_b[:], ident[:])
+        nc.vector.tensor_tensor(
+            out=dg[:],
+            in0=ident_b[:].unsqueeze(1).to_broadcast([P, G * T, P]),
+            in1=r_col[:].rearrange("p g t -> p (g t)").unsqueeze(2).to_broadcast([P, G * T, P]),
+            op=ALU.mult,
+        )
+        nc.vector.tensor_scalar(out=dn[:], in0=dg[:], scalar1=-1.0, scalar2=None, op0=ALU.mult)
+        ph_col = kt("ph_col", [P, G, T], BF16)
+        nc.vector.tensor_scalar(out=ph_col[:], in0=p_col[:], scalar1=0.5, scalar2=None, op0=ALU.mult)
+
+        ph_f32 = kt("ph_f32", [P, G, T], F32)
+        nc.vector.tensor_scalar(out=ph_f32[:], in0=p_col[:], scalar1=0.5, scalar2=None, op0=ALU.mult)
+
+        def cp(eng, dst, src):
+            if eng == "S":
+                nc.scalar.copy(dst, src)
+            else:
+                nc.vector.tensor_copy(dst, src)
+
+        def quant(codes, scales, in_):
+            nc.vector.quantize_mx(out=codes.bitcast(FP8X4), scales=scales, in_=in_)
+
+        wt = {}
+        a_codes = grid("a_codes", [P, N], U32, G, G)
+        a_scales = grid("a_scales", [P, N], U8, G, G)
+        hT = grid("hT", [P, N, T], BF16, H, G)
+        hp_codes = grid("hp_codes", [P, N], U32, H, G)
+        hp_scales = grid("hp_scales", [P, N], U8, H, G)
+        x_val = [kt("x_val%d" % g, [P, T, X], BF16) for g in range(H)]
+        x_codes = [kt("x_codes%d" % g, [P, N], U32) for g in range(H)]
+        x_scales = [kt("x_scales%d" % g, [P, N], U8) for g in range(H)]
+        win_codes = [kt("win_codes%d" % g, [P, N], U32) for g in range(G)]
+        win_scales = [kt("win_scales%d" % g, [P, N], U8) for g in range(G)]
+        v = grid("v", [P, T, N], F32, H, G)
+        u_codes = grid("u_codes", [P, N], U32, H, G)
+        u_scales = grid("u_scales", [P, N], U8, H, G)
+        bank = {}
+        a_mix = {}
+        hp_mix = {}
+        x_mix = {}
+        win_mix = {}
+        u_mix = {}
+        e = {}
+        o_tile = {}
+
+        def words_turn(key, words, lo, pair):
+            ps = bank[key] = psum.tile([P, 2, 2, P], F32, name="o", tag="bank", bufs=8)
+            for tt in range(2):
+                for u in range(2):
+                    nc.tensor.transpose(ps[:, u, tt, :], words[:, 2 * pair + tt, lo + u:lo + 256:2], ident[:])
+
+        def w(ng, gk, pair):
+            words_turn(("w", ng, gk, pair), w_nat[ng][:].bitcast(F32), 256 * gk, pair)
+
+        def W(eng, ng, gk, pair):
+            if (gk, ng) not in wt:
+                wt[gk, ng] = mix("wt", [P, 2, T, P, 2])
+            dst = wt[gk, ng][:, :, 2 * pair:2 * pair + 2, :, :].rearrange("p u t m e -> p u (t m e)").bitcast(F32)
+            cp(eng, dst, bank["w", ng, gk, pair][:].rearrange("p u t m -> p u (t m)"))
+
+        def a(gk, ng, tn):
+            ps = bank["a", gk, ng, tn] = psum.tile([P, T, P], F32, name="z", tag="bank", bufs=8)
+            for t in range(T):
+                nc.tensor.matmul(ps[:, t, :], dg[:, gk * T + t, :], w_nat[gk][:, t, N * ng + tn:N * (ng + 1):T], start=True, stop=False)
+                nc.tensor.matmul(ps[:, t, :], dn[:, gk * T + t, :], wt[gk, ng][:, t // 2, tn, :, t % 2], start=False, stop=True)
+
+        def A(eng, gk, ng, tn):
+            if (gk, ng) not in a_mix:
+                a_mix[gk, ng] = mix("a_mix", [P, T, P, T])
+            cp(eng, a_mix[gk, ng][:, tn, :, :], bank["a", gk, ng, tn][:].rearrange("p t m -> p m t"))
+
+        def aq(gk, ng):
+            quant(a_codes[gk, ng][:], a_scales[gk, ng][:], a_mix[gk, ng][:].rearrange("p a m t -> p (a m t)"))
+
+        def h_(g, gk, pair):
+            words_turn(("h", g, gk, pair), h_nat[g][:].bitcast(F32), 256 * gk, pair)
+
+        def H_(eng, g, gk, pair):
+            dst = hT[g, gk][:, 256 * pair:256 * (pair + 1), :].rearrange("p k t -> p (k t)").bitcast(F32)
+            cp(eng, dst.rearrange("p (k u) -> p k u", u=2), bank["h", g, gk, pair][:].rearrange("p u t m -> p (t m) u"))
+
+        def hg(g, gk):
+            hp_mix[g, gk] = mix("hp_mix", [P, N, T])
+            nc.vector.tensor_tensor(out=hp_mix[g, gk][:], in0=hT[g, gk][:], in1=p_col[:, gk, :].unsqueeze(1).to_broadcast([P, N, T]), op=ALU.mult)
+
+        def hq(g, gk):
+            quant(hp_codes[g, gk][:], hp_scales[g, gk][:], hp_mix[g, gk][:].rearrange("p k t -> p (k t)"))
+
+        def hh(g):
+            nc.vector.tensor_scalar(out=h_nat[g][:], in0=h_nat[g][:], scalar1=0.5, scalar2=None, op0=ALU.mult)
+
+        def xc(eng, g):
+            cp(eng, x_val[g][:], x_raw[g][:].bitcast(FP8))
+
+        def x_(g, pair):
+            words_turn(("x", g, pair), x_val[g][:].bitcast(F32), 0, pair)
+
+        def X_(g, pair):
+            if g not in x_mix:
+                x_mix[g] = mix("hp_mix", [P, N, T])
+            nc.vector.tensor_tensor(
+                out=x_mix[g][:, 256 * pair:256 * (pair + 1), :].rearrange("p k (u e) -> p k u e", e=2),
+                in0=bank["x", g, pair][:].rearrange("p u t m -> p u (t m)").bitcast(BF16).rearrange("p u (k e) -> p k u e", e=2),
+                in1=s_col[:].rearrange("p (u e) -> p u e", e=2).unsqueeze(1).to_broadcast([P, 256, 2, 2]),
+                op=ALU.mult,
+            )
+
+        def xq(g):
+            quant(x_codes[g][:], x_scales[g][:], x_mix[g][:].rearrange("p k t -> p (k t)"))
+
+        def wl(eng, ng):
+            win_mix[ng] = mix("win_mix", [P, T, P, T])
+            cp(eng, win_mix[ng][:], win_nat[:, :, N * ng:N * (ng + 1)].rearrange("p t (m a) -> p a m t", a=T))
+
+        def wq(ng):
+            quant(win_codes[ng][:], win_scales[ng][:], win_mix[ng][:].rearrange("p a m t -> p (a m t)"))
+
+        def drive(ps, g, ng, tn, codes, scales, lo, hi):
+            c = slice(tn * P, (tn + 1) * P)
+            k = slice(lo, hi)
+            nc.tensor.matmul_mx(ps, lhsT=win_codes[ng][:, c].bitcast(FP8X4), lhsT_scale=win_scales[ng][:, c],
+                                rhs=x_codes[g][:, k].bitcast(FP8X4), rhs_scale=x_scales[g][:, k], start=True, stop=False)
+            for gk in range(G):
+                nc.tensor.matmul_mx(ps, lhsT=a_codes[gk, ng][:, c].bitcast(FP8X4), lhsT_scale=a_scales[gk, ng][:, c],
+                                    rhs=codes[g, gk][:, k].bitcast(FP8X4), rhs_scale=scales[g, gk][:, k], start=False, stop=(gk == G - 1))
+
+        def s(g, ng, tn):
+            ps = bank["s", g, ng, tn] = psum.tile([P, N], F32, name="z", tag="bank", bufs=8)
+            drive(ps[:], g, ng, tn, hp_codes, hp_scales, 0, N)
+
+        def S(g, ng, tn):
+            nc.scalar.activation(v[g, ng][:, tn, :], bank["s", g, ng, tn][:], ACT.Tanh, bias=b_col[:, ng, tn:tn + 1])
+
+        def us(g, ng, half):
+            c = slice(2 * half, 2 * half + 2)
+            nc.vector.scalar_tensor_tensor(
+                out=v[g, ng][:, c, :], in0=hT[g, ng][:, :, c].rearrange("p k t -> p t k"), scalar=1.5,
+                in1=v[g, ng][:, c, :], op0=ALU.mult, op1=ALU.add)
+
+        def ug(g, ng):
+            u_mix[g, ng] = mix("u_mix", [P, N, T])
+            nc.vector.tensor_tensor(out=u_mix[g, ng][:], in0=v[g, ng][:].rearrange("p t k -> p k t"),
+                                    in1=ph_col[:, ng, :].unsqueeze(1).to_broadcast([P, N, T]), op=ALU.mult)
+
+        u_lin = {}
+
+        def ul(g, ng, tn):
+            if (g, ng) not in u_lin:
+                u_lin[g, ng] = mix("u_lin", [P, T, N])
+            nc.scalar.activation(u_lin[g, ng][:, tn, :], v[g, ng][:, tn, :], ACT.Copy, scale=ph_f32[:, ng, tn:tn + 1])
+
+        def ui(g, ng):
+            u_mix[g, ng] = mix("u_mix", [P, N, T])
+            nc.vector.tensor_copy(u_mix[g, ng][:], u_lin[g, ng][:].rearrange("p t k -> p k t"))
+
+        def uq(g, ng):
+            quant(u_codes[g, ng][:], u_scales[g, ng][:], u_mix[g, ng][:].rearrange("p k t -> p (k t)"))
+
+        def vs(g, ng):
+            nc.scalar.mul(v[g, ng][:], v[g, ng][:], 0.75)
+
+        def z(g, ng, tn, half, parts):
+            n = N // parts
+            ps = bank["z", g, ng, tn, half] = psum.tile([P, N], F32, name="z", tag="bank", bufs=8)
+            drive(ps[:, 0:n], g, ng, tn, u_codes, u_scales, n * half, n * (half + 1))
+
+        def Z(g, ng, tn, half, parts):
+            if (g, ng) not in e:
+                e[g, ng] = page("e", [P, T, N], F32)
+            n = N // parts
+            nc.scalar.activation(e[g, ng][:, tn, n * half:n * (half + 1)], bank["z", g, ng, tn, half][:, 0:n], ACT.Tanh, bias=b_col[:, ng, tn:tn + 1])
+
+        def cb(g, ng, tn, half, parts):
+            n = N // parts
+            k = slice(n * half, n * (half + 1))
+            nc.vector.scalar_tensor_tensor(out=e[g, ng][:, tn, k], in0=v[g, ng][:, tn, k], scalar=0.75, in1=e[g, ng][:, tn, k], op0=ALU.mult, op1=ALU.add)
+
+        def o(g, ng, j):
+            ps = bank["o", g, ng, j] = psum.tile([P, T, P], F32, name="o", tag="bank", bufs=8)
+            c = slice(P * j, P * (j + 1))
+            for tn in range(T):
+                if (g, ng) in ACC:
+                    nc.tensor.matmul(ps[:, tn, :], v[g, ng][:, tn, c], ident[:], start=True, stop=False, is_transpose=True)
+                    nc.tensor.matmul(ps[:, tn, :], e[g, ng][:, tn, c], ident[:], start=False, stop=True, is_transpose=True)
+                else:
+                    nc.tensor.transpose(ps[:, tn, :], e[g, ng][:, tn, c], ident[:])
+
+        def F(g, ng, j):
+            if (g, ng) not in o_tile:
+                o_tile[g, ng] = page("o_tile", [P, T, N], F32)
+            nc.vector.scalar_tensor_tensor(
+                out=o_tile[g, ng][:, j, :].rearrange("p (m t) -> p m t", t=T), in0=bank["o", g, ng, j][:].rearrange("p t m -> p m t"), scalar=0.25,
+                in1=h_nat[g][:, j, N * ng:N * (ng + 1)].rearrange("p (m t) -> p m t", t=T), op0=ALU.mult, op1=ALU.add)
+
+        def st(g, ng, lo, hi):
+            nc.sync.dma_start(out=out_rows[g, :, lo:hi, N * ng:N * (ng + 1)], in_=o_tile[g, ng][:, lo:hi, :])
+
+        step = dict(w=w, W=W, a=a, A=A, aq=aq, h_=h_, H_=H_, hg=hg, hq=hq, hh=hh, xc=xc, x_=x_, X_=X_, xq=xq, wl=wl, wq=wq,
+                    s=s, S=S, us=us, ug=ug, ul=ul, ui=ui, uq=uq, vs=vs, z=z, Z=Z, cb=cb, o=o, F=F, st=st)
+        for line in PLAN:
+            step[line[0]](*line[1:])
+
+
+PLAN = (
+    ("w", 0, 0, 0),
+    ("W", "S", 0, 0, 0),
+    ("w", 0, 0, 1),
+    ("W", "V", 0, 0, 1),
+    ("w", 0, 1, 0),
+    ("W", "S", 0, 1, 0),
+    ("w", 0, 1, 1),
+    ("W", "S", 0, 1, 1),
+    ("a", 0, 0, 1),
+    ("A", "S", 0, 0, 1),
+    ("h_", 0, 1, 0),
+    ("H_", "S", 0, 1, 0),
+    ("h_", 0, 1, 1),
+    ("H_", "V", 0, 1, 1),
+    ("hg", 0, 1),
+    ("h_", 0, 0, 0),
+    ("H_", "S", 0, 0, 0),
+    ("h_", 0, 0, 1),
+    ("H_", "S", 0, 0, 1),
+    ("hg", 0, 0),
+    ("hq", 0, 1),
+    ("w", 1, 0, 0),
+    ("W", "S", 1, 0, 0),
+    ("hq", 0, 0),
+    ("xc", "V", 0),
+    ("xc", "V", 1),
+    ("w", 1, 0, 1),
+    ("W", "S", 1, 0, 1),
+    ("w", 1, 1, 0),
+    ("a", 0, 0, 2),
+    ("a", 1, 0, 0),
+    ("W", "S", 1, 1, 0),
+    ("w", 1, 1, 1),
+    ("wl", "V", 0),
+    ("A", "S", 0, 0, 2),
+    ("A", "S", 1, 0, 0),
+    ("W", "S", 1, 1, 1),
+    ("a", 1, 0, 1),
+    ("a", 0, 0, 3),
+    ("A", "S", 1, 0, 1),
+    ("a", 0, 1, 3),
+    ("x_", 0, 1),
+    ("X_", 0, 1),
+    ("wl", "S", 1),
+    ("x_", 0, 0),
+    ("X_", 0, 0),
+    ("A", "S", 0, 0, 3),
+    ("a", 1, 0, 3),
+    ("A", "S", 1, 0, 3),
+    ("a", 1, 1, 0),
+    ("a", 0, 0, 0),
+    ("A", "S", 0, 0, 0),
+    ("a", 1, 0, 2),
+    ("a", 1, 1, 2),
+    ("wq", 0),
+    ("a", 1, 1, 3),
+    ("xq", 0),
+    ("A", "S", 0, 1, 3),
+    ("aq", 0, 0),
+    ("a", 0, 1, 1),
+    ("A", "S", 1, 0, 2),
+    ("x_", 1, 1),
+    ("X_", 1, 1),
+    ("x_", 1, 0),
+    ("X_", 1, 0),
+    ("A", "S", 1, 1, 2),
+    ("A", "S", 1, 1, 0),
+    ("A", "S", 0, 1, 1),
+    ("A", "S", 1, 1, 3),
+    ("h_", 1, 1, 0),
+    ("H_", "S", 1, 1, 0),
+    ("wq", 1),
+    ("aq", 1, 0),
+    ("a", 0, 1, 0),
+    ("h_", 1, 1, 1),
+    ("H_", "S", 1, 1, 1),
+    ("hg", 1, 1),
+    ("h_", 1, 0, 0),
+    ("H_", "S", 1, 0, 0),
+    ("a", 1, 1, 1),
+    ("A", "S", 1, 1, 1),
+    ("h_", 1, 0, 1),
+    ("H_", "S", 1, 0, 1),
+    ("hg", 1, 0),
+    ("a", 0, 1, 2),
+    ("s", 0, 0, 1),
+    ("A", "S", 0, 1, 2),
+    ("A", "S", 0, 1, 0),
+    ("s", 0, 0, 0),
+    ("S", 0, 0, 1),
+    ("S", 0, 0, 0),
+    ("aq", 1, 1),
+    ("s", 0, 0, 2),
+    ("S", 0, 0, 2),
+    ("s", 0, 0, 3),
+    ("S", 0, 0, 3),
+    ("aq", 0, 1),
+    ("s", 0, 1, 3),
+    ("s", 0, 1, 2),
+    ("s", 0, 1, 1),
+    ("s", 0, 1, 0),
+    ("us", 0, 0, 0),
+    ("hq", 1, 0),
+    ("us", 0, 0, 1),
+    ("hq", 1, 1),
+    ("ul", 0, 0, 1),
+    ("S", 0, 1, 3),
+    ("S", 0, 1, 2),
+    ("xq", 1),
+    ("s", 1, 1, 3),
+    ("s", 1, 0, 0),
+    ("s", 1, 0, 3),
+    ("s", 1, 0, 1),
+    ("ul", 0, 0, 2),
+    ("S", 0, 1, 1),
+    ("S", 0, 1, 0),
+    ("us", 0, 1, 1),
+    ("ul", 0, 0, 0),
+    ("us", 0, 1, 0),
+    ("ul", 0, 0, 3),
+    ("vs", 0, 0),
+    ("ui", 0, 0),
+    ("ug", 0, 1),
+    ("s", 1, 0, 2),
+    ("S", 1, 0, 1),
+    ("S", 1, 0, 2),
+    ("s", 1, 1, 0),
+    ("S", 1, 1, 0),
+    ("s", 1, 1, 1),
+    ("s", 1, 1, 2),
+    ("S", 1, 1, 1),
+    ("S", 1, 1, 3),
+    ("S", 1, 0, 3),
+    ("uq", 0, 0),
+    ("uq", 0, 1),
+    ("z", 0, 0, 3, 0, 1),
+    ("z", 0, 0, 2, 0, 1),
+    ("z", 0, 0, 0, 0, 1),
+    ("S", 1, 1, 2),
+    ("us", 1, 1, 0),
+    ("z", 0, 0, 1, 0, 1),
+    ("z", 0, 1, 1, 0, 1),
+    ("S", 1, 0, 0),
+    ("Z", 0, 0, 2, 0, 1),
+    ("us", 1, 0, 1),
+    ("us", 1, 1, 1),
+    ("ul", 1, 0, 2),
+    ("us", 1, 0, 0),
+    ("z", 0, 1, 0, 0, 1),
+    ("z", 0, 1, 3, 0, 1),
+    ("Z", 0, 0, 0, 0, 1),
+    ("ug", 1, 1),
+    ("Z", 0, 0, 3, 0, 1),
+    ("Z", 0, 0, 1, 0, 1),
+    ("o", 0, 0, 1),
+    ("o", 0, 0, 2),
+    ("o", 0, 0, 0),
+    ("o", 0, 0, 3),
+    ("ul", 1, 0, 3),
+    ("ul", 1, 0, 0),
+    ("ul", 1, 0, 1),
+    ("ui", 1, 0),
+    ("uq", 1, 1),
+    ("Z", 0, 1, 3, 0, 1),
+    ("Z", 0, 1, 1, 0, 1),
+    ("z", 0, 1, 2, 0, 1),
+    ("vs", 1, 0),
+    ("uq", 1, 0),
+    ("Z", 0, 1, 0, 0, 1),
+    ("hh", 0),
+    ("F", 0, 0, 0),
+    ("F", 0, 0, 1),
+    ("z", 1, 1, 3, 1, 2),
+    ("Z", 1, 1, 3, 1, 2),
+    ("z", 1, 0, 2, 0, 1),
+    ("Z", 1, 0, 2, 0, 1),
+    ("z", 1, 1, 3, 0, 2),
+    ("Z", 1, 1, 3, 0, 2),
+    ("cb", 1, 1, 3, 0, 2),
+    ("z", 1, 1, 2, 1, 2),
+    ("Z", 1, 1, 2, 1, 2),
+    ("cb", 1, 1, 2, 1, 2),
+    ("z", 1, 1, 1, 0, 2),
+    ("Z", 1, 1, 1, 0, 2),
+    ("st", 0, 0, 0, 2),
+    ("z", 1, 1, 0, 0, 2),
+    ("cb", 1, 1, 3, 1, 2),
+    ("cb", 1, 1, 1, 0, 2),
+    ("F", 0, 0, 3),
+    ("Z", 0, 1, 2, 0, 1),
+    ("z", 1, 1, 0, 1, 2),
+    ("Z", 1, 1, 0, 1, 2),
+    ("F", 0, 0, 2),
+    ("st", 0, 0, 2, 4),
+    ("cb", 1, 1, 0, 1, 2),
+    ("z", 1, 1, 1, 1, 2),
+    ("z", 1, 0, 1, 0, 1),
+    ("Z", 1, 1, 0, 0, 2),
+    ("cb", 1, 1, 0, 0, 2),
+    ("z", 1, 0, 3, 0, 1),
+    ("Z", 1, 1, 1, 1, 2),
+    ("cb", 1, 1, 1, 1, 2),
+    ("z", 1, 1, 2, 0, 2),
+    ("Z", 1, 0, 1, 0, 1),
+    ("hh", 1),
+    ("Z", 1, 0, 3, 0, 1),
+    ("z", 1, 0, 0, 0, 1),
+    ("o", 1, 1, 2),
+    ("Z", 1, 1, 2, 0, 2),
+    ("cb", 1, 1, 2, 0, 2),
+    ("o", 1, 1, 1),
+    ("F", 1, 1, 2),
+    ("st", 1, 1, 2, 3),
+    ("Z", 1, 0, 0, 0, 1),
+    ("o", 1, 0, 2),
+    ("o", 1, 0, 3),
+    ("o", 1, 0, 1),
+    ("o", 1, 1, 0),
+    ("F", 1, 1, 1),
+    ("st", 1, 1, 1, 2),
+    ("F", 1, 0, 2),
+    ("F", 1, 0, 3),
+    ("F", 1, 0, 1),
+    ("st", 1, 0, 2, 4),
+    ("o", 1, 0, 0),
+    ("F", 1, 1, 0),
+    ("st", 1, 1, 0, 1),
+    ("F", 1, 0, 0),
+    ("st", 1, 0, 0, 2),
+    ("vs", 0, 1),
+    ("o", 0, 1, 2),
+    ("F", 0, 1, 2),
+    ("o", 0, 1, 3),
+    ("F", 0, 1, 3),
+    ("st", 0, 1, 2, 4),
+    ("o", 0, 1, 1),
+    ("F", 0, 1, 1),
+    ("o", 0, 1, 0),
+    ("F", 0, 1, 0),
+    ("st", 0, 1, 0, 2),
+    ("o", 1, 1, 3),
+    ("F", 1, 1, 3),
+    ("st", 1, 1, 3, 4),
+)

@@ -18,7 +18,7 @@ T = 4
 N = P * T
 G = D // N
 H = B // N
-ACC = ((0, 0), (0, 1), (1, 0),)
+ACC = ((0, 0),)
 FLOPS = 2 * B * D * (X + 2 * D)
 
 
@@ -42,14 +42,20 @@ def tile_antisymmetricssprk2step_kernel(tc, h, x_bytes, x_scale, w, win, b, p, r
         def grid(name, shape, dtype, na, nb):
             return {(i, j): kt("%s%d%d" % (name, i, j), shape, dtype) for i in range(na) for j in range(nb)}
 
+        u_codes = grid("u_codes", [P, N], U32, H, G)
+        u_scales = grid("u_scales", [P, N], U8, H, G)
+        warm_codes = u_codes[1, 1]
+        warm_scales = u_scales[1, 1]
+        nc.vector.memset(warm_codes[:], 0)
+        nc.vector.memset(warm_scales[:].bitcast(U32), 0)
         r_col = kt("r_col", [P, G, T], BF16)
         p_col = kt("p_col", [P, G, T], BF16)
         b_col = kt("b_col", [P, G, T], BF16)
         s_col = kt("s_col", [P, T], F32)
         nc.scalar.dma_start(out=r_col[:], in_=r.rearrange("(g p t) -> p g t", p=P, t=T))
         nc.scalar.dma_start(out=p_col[:], in_=p.rearrange("(g p t) -> p g t", p=P, t=T))
-        nc.gpsimd.dma_start(out=s_col[:], in_=x_scale.rearrange("o (p t) -> p (o t)", p=P, t=T))
-        nc.gpsimd.dma_start(out=b_col[:], in_=b.rearrange("(g p t) -> p g t", p=P, t=T))
+        nc.scalar.dma_start(out=s_col[:], in_=x_scale.rearrange("o (p t) -> p (o t)", p=P, t=T))
+        nc.scalar.dma_start(out=b_col[:], in_=b.rearrange("(g p t) -> p g t", p=P, t=T))
 
         w_rows = w.rearrange("(g p t) c -> g p t c", p=P, t=T)
         h_rows = h.rearrange("(g p t) c -> g p t c", p=P, t=T)
@@ -59,11 +65,10 @@ def tile_antisymmetricssprk2step_kernel(tc, h, x_bytes, x_scale, w, win, b, p, r
         h_nat = [kt("h_nat%d" % g, [P, T, D], BF16) for g in range(H)]
         x_raw = [kt("x_raw%d" % g, [P, T, X], U8) for g in range(H)]
         win_nat = page("win_nat", [P, T, D], BF16)
-        for t in range(T):
-            nc.sync.dma_start(out=w_nat[0][:, t:t + 1, :], in_=w_rows[0, :, t:t + 1, :])
-        nc.sync.dma_start(out=h_nat[0][:], in_=h_rows[0])
         for t in range(0, T, 2):
-            nc.sync.dma_start(out=w_nat[1][:, t:t + 2, :], in_=w_rows[1, :, t:t + 2, :])
+            nc.sync.dma_start(out=h_nat[0][:, t:t + 2, :], in_=h_rows[0, :, t:t + 2, :])
+        for g in range(G):
+            nc.sync.dma_start(out=w_nat[g][:], in_=w_rows[g])
         nc.sync.dma_start(out=x_raw[0][:], in_=x_rows[0])
         nc.sync.dma_start(out=win_nat[:], in_=win.rearrange("(p t) c -> p t c", p=P, t=T))
         nc.sync.dma_start(out=x_raw[1][:], in_=x_rows[1])
@@ -112,8 +117,6 @@ def tile_antisymmetricssprk2step_kernel(tc, h, x_bytes, x_scale, w, win, b, p, r
         win_codes = [kt("win_codes%d" % g, [P, N], U32) for g in range(G)]
         win_scales = [kt("win_scales%d" % g, [P, N], U8) for g in range(G)]
         v = grid("v", [P, T, N], F32, H, G)
-        u_codes = grid("u_codes", [P, N], U32, H, G)
-        u_scales = grid("u_scales", [P, N], U8, H, G)
         bank = {}
         a_mix = {}
         hp_mix = {}
@@ -123,31 +126,43 @@ def tile_antisymmetricssprk2step_kernel(tc, h, x_bytes, x_scale, w, win, b, p, r
         e = {}
         o_tile = {}
 
+
+        def dm(passes):
+            ps = psum.tile([P, N], F32, name="z", tag="bank", bufs=8)
+            for i in range(passes):
+                nc.tensor.matmul_mx(ps[:], lhsT=warm_codes[:, 0:P].bitcast(FP8X4), lhsT_scale=warm_scales[:, 0:P],
+                                    rhs=warm_codes[:].bitcast(FP8X4), rhs_scale=warm_scales[:], start=True, stop=True)
+
+        dm(7)
+
         def words_turn(key, words, lo, pair):
             ps = bank[key] = psum.tile([P, 2, 2, P], F32, name="o", tag="bank", bufs=8)
             for tt in range(2):
                 for u in range(2):
                     nc.tensor.transpose(ps[:, u, tt, :], words[:, 2 * pair + tt, lo + u:lo + 256:2], ident[:])
 
-        def w(ng, gk, pair):
-            words_turn(("w", ng, gk, pair), w_nat[ng][:].bitcast(F32), 256 * gk, pair)
+        def w(ng, gk, u):
+            ps = bank["w", ng, gk, u] = psum.tile([P, T, P], F32, name="o", tag="bank", bufs=8)
+            for tn in range(T):
+                nc.tensor.transpose(ps[:, tn, :], w_nat[ng][:, tn, :].bitcast(F32)[:, 256 * gk + u:256 * (gk + 1):2], ident[:])
 
-        def W(eng, ng, gk, pair):
+        def W(eng, ng, gk, u):
             if (gk, ng) not in wt:
-                wt[gk, ng] = mix("wt", [P, 2, T, P, 2])
-            dst = wt[gk, ng][:, :, 2 * pair:2 * pair + 2, :, :].rearrange("p u t m e -> p u (t m e)").bitcast(F32)
-            cp(eng, dst, bank["w", ng, gk, pair][:].rearrange("p u t m -> p u (t m)"))
+                wt[gk, ng] = mix("wt", [P, 2, N, 2])
+            dst = wt[gk, ng][:, u, :, :].rearrange("p n e -> p (n e)").bitcast(F32)
+            cp(eng, dst.rearrange("p (m t) -> p m t", t=T), bank["w", ng, gk, u][:].rearrange("p t m -> p m t"))
 
-        def a(gk, ng, tn):
-            ps = bank["a", gk, ng, tn] = psum.tile([P, T, P], F32, name="z", tag="bank", bufs=8)
+        def a(gk, ng, q):
+            ps = bank["a", gk, ng, q] = psum.tile([P, T, P], F32, name="z", tag="bank", bufs=8)
             for t in range(T):
-                nc.tensor.matmul(ps[:, t, :], dg[:, gk * T + t, :], w_nat[gk][:, t, N * ng + tn:N * (ng + 1):T], start=True, stop=False)
-                nc.tensor.matmul(ps[:, t, :], dn[:, gk * T + t, :], wt[gk, ng][:, t // 2, tn, :, t % 2], start=False, stop=True)
+                nc.tensor.matmul(ps[:, t, :], dg[:, gk * T + t, :], w_nat[gk][:, t, N * ng + P * q:N * ng + P * (q + 1)], start=True, stop=False)
+                nc.tensor.matmul(ps[:, t, :], dn[:, gk * T + t, :], wt[gk, ng][:, t // 2, P * q:P * (q + 1), t % 2], start=False, stop=True)
 
-        def A(eng, gk, ng, tn):
+        def A(eng, gk, ng, q):
             if (gk, ng) not in a_mix:
                 a_mix[gk, ng] = mix("a_mix", [P, T, P, T])
-            cp(eng, a_mix[gk, ng][:, tn, :, :], bank["a", gk, ng, tn][:].rearrange("p t m -> p m t"))
+            m = P // T
+            cp(eng, a_mix[gk, ng][:, :, m * q:m * (q + 1), :], bank["a", gk, ng, q][:].rearrange("p t (m a) -> p a m t", a=T))
 
         def aq(gk, ng):
             quant(a_codes[gk, ng][:], a_scales[gk, ng][:], a_mix[gk, ng][:].rearrange("p a m t -> p (a m t)"))
@@ -276,253 +291,270 @@ def tile_antisymmetricssprk2step_kernel(tc, h, x_bytes, x_scale, w, win, b, p, r
             nc.sync.dma_start(out=out_rows[g, :, lo:hi, N * ng:N * (ng + 1)], in_=o_tile[g, ng][:, lo:hi, :])
 
         step = dict(w=w, W=W, a=a, A=A, aq=aq, h_=h_, H_=H_, hg=hg, hq=hq, hh=hh, xc=xc, x_=x_, X_=X_, xq=xq, wl=wl, wq=wq,
-                    s=s, S=S, us=us, ug=ug, ul=ul, ui=ui, uq=uq, vs=vs, z=z, Z=Z, cb=cb, o=o, F=F, st=st)
+                    dm=dm, s=s, S=S, us=us, ug=ug, ul=ul, ui=ui, uq=uq, vs=vs, z=z, Z=Z, cb=cb, o=o, F=F, st=st)
         for line in PLAN:
             step[line[0]](*line[1:])
 
 
 PLAN = (
+    ("h_", 0, 0, 0),
+    ("H_", "S", 0, 0, 0),
+    ("h_", 0, 1, 0),
+    ("H_", "V", 0, 1, 0),
+    ("h_", 0, 0, 1),
+    ("H_", "S", 0, 0, 1),
+    ("h_", 0, 1, 1),
+    ("H_", "S", 0, 1, 1),
+    ("hh", 0),
+    ("hg", 0, 1),
+    ("dm", 2),
     ("w", 0, 0, 0),
-    ("W", "S", 0, 0, 0),
+    ("W", "V", 0, 0, 0),
     ("w", 0, 0, 1),
-    ("W", "V", 0, 0, 1),
+    ("W", "S", 0, 0, 1),
     ("w", 0, 1, 0),
     ("W", "S", 0, 1, 0),
+    ("a", 0, 0, 0),
+    ("A", "S", 0, 0, 0),
     ("w", 0, 1, 1),
     ("W", "S", 0, 1, 1),
     ("a", 0, 0, 1),
-    ("A", "S", 0, 0, 1),
-    ("h_", 0, 1, 0),
-    ("H_", "S", 0, 1, 0),
-    ("h_", 0, 1, 1),
-    ("H_", "V", 0, 1, 1),
-    ("hg", 0, 1),
-    ("h_", 0, 0, 0),
-    ("H_", "S", 0, 0, 0),
-    ("h_", 0, 0, 1),
-    ("H_", "S", 0, 0, 1),
-    ("hg", 0, 0),
-    ("hq", 0, 1),
-    ("w", 1, 0, 0),
-    ("W", "S", 1, 0, 0),
-    ("hq", 0, 0),
-    ("xc", "V", 0),
-    ("xc", "V", 1),
-    ("w", 1, 0, 1),
-    ("W", "S", 1, 0, 1),
-    ("w", 1, 1, 0),
     ("a", 0, 0, 2),
-    ("a", 1, 0, 0),
-    ("W", "S", 1, 1, 0),
-    ("w", 1, 1, 1),
-    ("wl", "V", 0),
+    ("A", "S", 0, 0, 1),
     ("A", "S", 0, 0, 2),
-    ("A", "S", 1, 0, 0),
-    ("W", "S", 1, 1, 1),
-    ("a", 1, 0, 1),
-    ("a", 0, 0, 3),
-    ("A", "S", 1, 0, 1),
-    ("a", 0, 1, 3),
-    ("x_", 0, 1),
-    ("X_", 0, 1),
-    ("wl", "S", 1),
+    ("hg", 0, 0),
+    ("xc", "V", 0),
+    ("hq", 0, 0),
+    ("wl", "V", 1),
+    ("wq", 1),
+    ("hq", 0, 1),
+    ("xc", "S", 1),
+    ("wl", "V", 0),
+    ("wq", 0),
     ("x_", 0, 0),
     ("X_", 0, 0),
+    ("x_", 0, 1),
+    ("a", 0, 0, 3),
     ("A", "S", 0, 0, 3),
+    ("X_", 0, 1),
+    ("xq", 0),
+    ("a", 1, 0, 0),
+    ("A", "S", 1, 0, 0),
+    ("w", 1, 0, 0),
+    ("W", "S", 1, 0, 0),
+    ("w", 1, 0, 1),
+    ("W", "S", 1, 0, 1),
+    ("a", 1, 0, 1),
+    ("A", "S", 1, 0, 1),
+    ("a", 1, 0, 2),
+    ("A", "S", 1, 0, 2),
+    ("w", 1, 1, 0),
+    ("W", "S", 1, 1, 0),
+    ("w", 1, 1, 1),
+    ("W", "V", 1, 1, 1),
     ("a", 1, 0, 3),
     ("A", "S", 1, 0, 3),
-    ("a", 1, 1, 0),
-    ("a", 0, 0, 0),
-    ("A", "S", 0, 0, 0),
-    ("a", 1, 0, 2),
-    ("a", 1, 1, 2),
-    ("wq", 0),
-    ("a", 1, 1, 3),
-    ("xq", 0),
-    ("A", "S", 0, 1, 3),
-    ("aq", 0, 0),
-    ("a", 0, 1, 1),
-    ("A", "S", 1, 0, 2),
-    ("x_", 1, 1),
-    ("X_", 1, 1),
-    ("x_", 1, 0),
-    ("X_", 1, 0),
-    ("A", "S", 1, 1, 2),
-    ("A", "S", 1, 1, 0),
-    ("A", "S", 0, 1, 1),
-    ("A", "S", 1, 1, 3),
+    ("a", 0, 1, 0),
+    ("A", "S", 0, 1, 0),
+    ("h_", 1, 0, 0),
+    ("H_", "V", 1, 0, 0),
     ("h_", 1, 1, 0),
     ("H_", "S", 1, 1, 0),
-    ("wq", 1),
+    ("a", 0, 1, 1),
+    ("A", "S", 0, 1, 1),
+    ("a", 0, 1, 2),
+    ("A", "S", 0, 1, 2),
+    ("aq", 0, 0),
     ("aq", 1, 0),
-    ("a", 0, 1, 0),
-    ("h_", 1, 1, 1),
-    ("H_", "S", 1, 1, 1),
-    ("hg", 1, 1),
-    ("h_", 1, 0, 0),
-    ("H_", "S", 1, 0, 0),
-    ("a", 1, 1, 1),
-    ("A", "S", 1, 1, 1),
+    ("x_", 1, 0),
+    ("X_", 1, 0),
+    ("x_", 1, 1),
+    ("X_", 1, 1),
+    ("xq", 1),
+    ("a", 0, 1, 3),
+    ("A", "S", 0, 1, 3),
+    ("aq", 0, 1),
+    ("a", 1, 1, 0),
+    ("A", "S", 1, 1, 0),
     ("h_", 1, 0, 1),
     ("H_", "S", 1, 0, 1),
     ("hg", 1, 0),
-    ("a", 0, 1, 2),
-    ("s", 0, 0, 1),
-    ("A", "S", 0, 1, 2),
-    ("A", "S", 0, 1, 0),
-    ("s", 0, 0, 0),
-    ("S", 0, 0, 1),
-    ("S", 0, 0, 0),
+    ("hq", 1, 0),
+    ("h_", 1, 1, 1),
+    ("H_", "S", 1, 1, 1),
+    ("hg", 1, 1),
+    ("a", 1, 1, 1),
+    ("A", "S", 1, 1, 1),
+    ("a", 1, 1, 2),
+    ("A", "S", 1, 1, 2),
+    ("a", 1, 1, 3),
+    ("A", "S", 1, 1, 3),
     ("aq", 1, 1),
+    ("s", 0, 0, 0),
+    ("S", 0, 0, 0),
+    ("s", 0, 0, 1),
+    ("S", 0, 0, 1),
+    ("us", 0, 0, 0),
     ("s", 0, 0, 2),
     ("S", 0, 0, 2),
+    ("hq", 1, 1),
     ("s", 0, 0, 3),
     ("S", 0, 0, 3),
-    ("aq", 0, 1),
-    ("s", 0, 1, 3),
-    ("s", 0, 1, 2),
-    ("s", 0, 1, 1),
     ("s", 0, 1, 0),
-    ("us", 0, 0, 0),
-    ("hq", 1, 0),
+    ("s", 0, 1, 1),
+    ("s", 0, 1, 2),
+    ("s", 0, 1, 3),
     ("us", 0, 0, 1),
-    ("hq", 1, 1),
-    ("ul", 0, 0, 1),
-    ("S", 0, 1, 3),
-    ("S", 0, 1, 2),
-    ("xq", 1),
-    ("s", 1, 1, 3),
-    ("s", 1, 0, 0),
-    ("s", 1, 0, 3),
-    ("s", 1, 0, 1),
-    ("ul", 0, 0, 2),
-    ("S", 0, 1, 1),
-    ("S", 0, 1, 0),
-    ("us", 0, 1, 1),
+    ("hh", 1),
     ("ul", 0, 0, 0),
+    ("ul", 0, 0, 1),
+    ("S", 0, 1, 0),
+    ("S", 0, 1, 1),
     ("us", 0, 1, 0),
+    ("S", 0, 1, 2),
+    ("S", 0, 1, 3),
+    ("us", 0, 1, 1),
+    ("ul", 0, 0, 2),
     ("ul", 0, 0, 3),
-    ("vs", 0, 0),
     ("ui", 0, 0),
     ("ug", 0, 1),
-    ("s", 1, 0, 2),
+    ("uq", 0, 0),
+    ("s", 1, 0, 0),
+    ("S", 1, 0, 0),
+    ("s", 1, 0, 1),
     ("S", 1, 0, 1),
+    ("us", 1, 0, 0),
+    ("s", 1, 0, 2),
     ("S", 1, 0, 2),
+    ("uq", 0, 1),
+    ("vs", 0, 0),
+    ("s", 1, 0, 3),
+    ("S", 1, 0, 3),
+    ("us", 1, 0, 1),
     ("s", 1, 1, 0),
     ("S", 1, 1, 0),
     ("s", 1, 1, 1),
     ("s", 1, 1, 2),
     ("S", 1, 1, 1),
-    ("S", 1, 1, 3),
-    ("S", 1, 0, 3),
-    ("uq", 0, 0),
-    ("uq", 0, 1),
-    ("z", 0, 0, 3, 0, 1),
-    ("z", 0, 0, 2, 0, 1),
-    ("z", 0, 0, 0, 0, 1),
-    ("S", 1, 1, 2),
     ("us", 1, 1, 0),
-    ("z", 0, 0, 1, 0, 1),
-    ("z", 0, 1, 1, 0, 1),
-    ("S", 1, 0, 0),
-    ("Z", 0, 0, 2, 0, 1),
-    ("us", 1, 0, 1),
+    ("s", 1, 1, 3),
+    ("S", 1, 1, 2),
+    ("S", 1, 1, 3),
     ("us", 1, 1, 1),
-    ("ul", 1, 0, 2),
-    ("us", 1, 0, 0),
-    ("z", 0, 1, 0, 0, 1),
-    ("z", 0, 1, 3, 0, 1),
-    ("Z", 0, 0, 0, 0, 1),
-    ("ug", 1, 1),
-    ("Z", 0, 0, 3, 0, 1),
-    ("Z", 0, 0, 1, 0, 1),
-    ("o", 0, 0, 1),
-    ("o", 0, 0, 2),
-    ("o", 0, 0, 0),
-    ("o", 0, 0, 3),
-    ("ul", 1, 0, 3),
     ("ul", 1, 0, 0),
     ("ul", 1, 0, 1),
+    ("ul", 1, 0, 2),
+    ("ul", 1, 0, 3),
     ("ui", 1, 0),
-    ("uq", 1, 1),
-    ("Z", 0, 1, 3, 0, 1),
-    ("Z", 0, 1, 1, 0, 1),
-    ("z", 0, 1, 2, 0, 1),
-    ("vs", 1, 0),
     ("uq", 1, 0),
+    ("ul", 1, 1, 0),
+    ("ul", 1, 1, 1),
+    ("ul", 1, 1, 2),
+    ("ul", 1, 1, 3),
+    ("ui", 1, 1),
+    ("uq", 1, 1),
+    ("z", 0, 0, 0, 0, 1),
+    ("Z", 0, 0, 0, 0, 1),
+    ("z", 0, 0, 1, 0, 1),
+    ("Z", 0, 0, 1, 0, 1),
+    ("z", 0, 0, 2, 0, 1),
+    ("Z", 0, 0, 2, 0, 1),
+    ("z", 0, 0, 3, 0, 1),
+    ("Z", 0, 0, 3, 0, 1),
+    ("z", 0, 1, 0, 0, 1),
     ("Z", 0, 1, 0, 0, 1),
-    ("hh", 0),
+    ("cb", 0, 1, 0, 0, 1),
+    ("z", 0, 1, 1, 0, 1),
+    ("Z", 0, 1, 1, 0, 1),
+    ("cb", 0, 1, 1, 0, 1),
+    ("z", 0, 1, 2, 0, 1),
+    ("Z", 0, 1, 2, 0, 1),
+    ("cb", 0, 1, 2, 0, 1),
+    ("z", 0, 1, 3, 0, 1),
+    ("Z", 0, 1, 3, 0, 1),
+    ("cb", 0, 1, 3, 0, 1),
+    ("o", 0, 0, 0),
     ("F", 0, 0, 0),
+    ("st", 0, 0, 0, 1),
+    ("o", 0, 0, 1),
     ("F", 0, 0, 1),
-    ("z", 1, 1, 3, 1, 2),
-    ("Z", 1, 1, 3, 1, 2),
+    ("st", 0, 0, 1, 2),
+    ("z", 1, 0, 0, 0, 1),
+    ("Z", 1, 0, 0, 0, 1),
+    ("cb", 1, 0, 0, 0, 1),
+    ("z", 1, 0, 1, 0, 1),
+    ("Z", 1, 0, 1, 0, 1),
+    ("cb", 1, 0, 1, 0, 1),
+    ("o", 0, 0, 2),
+    ("F", 0, 0, 2),
+    ("st", 0, 0, 2, 3),
+    ("o", 0, 0, 3),
+    ("F", 0, 0, 3),
+    ("st", 0, 0, 3, 4),
     ("z", 1, 0, 2, 0, 1),
     ("Z", 1, 0, 2, 0, 1),
+    ("cb", 1, 0, 2, 0, 1),
+    ("z", 1, 0, 3, 0, 1),
+    ("o", 0, 1, 0),
+    ("o", 0, 1, 1),
+    ("F", 0, 1, 0),
+    ("F", 0, 1, 1),
+    ("Z", 1, 0, 3, 0, 1),
+    ("cb", 1, 0, 3, 0, 1),
+    ("st", 0, 1, 0, 1),
+    ("st", 0, 1, 1, 2),
+    ("z", 1, 1, 0, 0, 2),
+    ("Z", 1, 1, 0, 0, 2),
+    ("cb", 1, 1, 0, 0, 2),
+    ("z", 1, 1, 1, 0, 2),
+    ("Z", 1, 1, 1, 0, 2),
+    ("cb", 1, 1, 1, 0, 2),
+    ("z", 1, 1, 2, 0, 2),
+    ("Z", 1, 1, 2, 0, 2),
+    ("cb", 1, 1, 2, 0, 2),
     ("z", 1, 1, 3, 0, 2),
+    ("o", 0, 1, 2),
+    ("o", 0, 1, 3),
+    ("F", 0, 1, 2),
+    ("F", 0, 1, 3),
+    ("o", 1, 0, 0),
+    ("o", 1, 0, 1),
     ("Z", 1, 1, 3, 0, 2),
     ("cb", 1, 1, 3, 0, 2),
+    ("st", 0, 1, 2, 3),
+    ("st", 0, 1, 3, 4),
+    ("F", 1, 0, 0),
+    ("st", 1, 0, 0, 1),
+    ("F", 1, 0, 1),
+    ("st", 1, 0, 1, 2),
+    ("z", 1, 1, 0, 1, 2),
+    ("Z", 1, 1, 0, 1, 2),
+    ("cb", 1, 1, 0, 1, 2),
+    ("z", 1, 1, 1, 1, 2),
+    ("Z", 1, 1, 1, 1, 2),
+    ("cb", 1, 1, 1, 1, 2),
     ("z", 1, 1, 2, 1, 2),
     ("Z", 1, 1, 2, 1, 2),
     ("cb", 1, 1, 2, 1, 2),
-    ("z", 1, 1, 1, 0, 2),
-    ("Z", 1, 1, 1, 0, 2),
-    ("st", 0, 0, 0, 2),
-    ("z", 1, 1, 0, 0, 2),
-    ("cb", 1, 1, 3, 1, 2),
-    ("cb", 1, 1, 1, 0, 2),
-    ("F", 0, 0, 3),
-    ("Z", 0, 1, 2, 0, 1),
-    ("z", 1, 1, 0, 1, 2),
-    ("Z", 1, 1, 0, 1, 2),
-    ("F", 0, 0, 2),
-    ("st", 0, 0, 2, 4),
-    ("cb", 1, 1, 0, 1, 2),
-    ("z", 1, 1, 1, 1, 2),
-    ("z", 1, 0, 1, 0, 1),
-    ("Z", 1, 1, 0, 0, 2),
-    ("cb", 1, 1, 0, 0, 2),
-    ("z", 1, 0, 3, 0, 1),
-    ("Z", 1, 1, 1, 1, 2),
-    ("cb", 1, 1, 1, 1, 2),
-    ("z", 1, 1, 2, 0, 2),
-    ("Z", 1, 0, 1, 0, 1),
-    ("hh", 1),
-    ("Z", 1, 0, 3, 0, 1),
-    ("z", 1, 0, 0, 0, 1),
-    ("o", 1, 1, 2),
-    ("Z", 1, 1, 2, 0, 2),
-    ("cb", 1, 1, 2, 0, 2),
-    ("o", 1, 1, 1),
-    ("F", 1, 1, 2),
-    ("st", 1, 1, 2, 3),
-    ("Z", 1, 0, 0, 0, 1),
+    ("z", 1, 1, 3, 1, 2),
     ("o", 1, 0, 2),
     ("o", 1, 0, 3),
-    ("o", 1, 0, 1),
     ("o", 1, 1, 0),
-    ("F", 1, 1, 1),
-    ("st", 1, 1, 1, 2),
+    ("o", 1, 1, 1),
+    ("Z", 1, 1, 3, 1, 2),
+    ("cb", 1, 1, 3, 1, 2),
+    ("o", 1, 1, 2),
+    ("o", 1, 1, 3),
     ("F", 1, 0, 2),
+    ("st", 1, 0, 2, 3),
     ("F", 1, 0, 3),
-    ("F", 1, 0, 1),
-    ("st", 1, 0, 2, 4),
-    ("o", 1, 0, 0),
+    ("st", 1, 0, 3, 4),
     ("F", 1, 1, 0),
     ("st", 1, 1, 0, 1),
-    ("F", 1, 0, 0),
-    ("st", 1, 0, 0, 2),
-    ("vs", 0, 1),
-    ("o", 0, 1, 2),
-    ("F", 0, 1, 2),
-    ("o", 0, 1, 3),
-    ("F", 0, 1, 3),
-    ("st", 0, 1, 2, 4),
-    ("o", 0, 1, 1),
-    ("F", 0, 1, 1),
-    ("o", 0, 1, 0),
-    ("F", 0, 1, 0),
-    ("st", 0, 1, 0, 2),
-    ("o", 1, 1, 3),
+    ("F", 1, 1, 1),
+    ("st", 1, 1, 1, 2),
+    ("F", 1, 1, 2),
+    ("st", 1, 1, 2, 3),
     ("F", 1, 1, 3),
     ("st", 1, 1, 3, 4),
 )

@@ -65,8 +65,9 @@ def tile_antisymmetricssprk2step_kernel(tc, h, x_bytes, x_scale, w, win, b, p, r
         h_nat = [kt("h_nat%d" % g, [P, T, D], BF16) for g in range(H)]
         x_raw = [kt("x_raw%d" % g, [P, T, X], U8) for g in range(H)]
         win_nat = page("win_nat", [P, T, D], BF16)
-        for t in range(0, T, 2):
-            nc.sync.dma_start(out=h_nat[0][:, t:t + 2, :], in_=h_rows[0, :, t:t + 2, :])
+        nc.sync.dma_start(out=h_nat[0][:, 0:1, :], in_=h_rows[0, :, 0:1, :])
+        nc.sync.dma_start(out=h_nat[0][:, 1:2, :], in_=h_rows[0, :, 1:2, :])
+        nc.sync.dma_start(out=h_nat[0][:, 2:4, :], in_=h_rows[0, :, 2:4, :])
         for g in range(G):
             nc.sync.dma_start(out=w_nat[g][:], in_=w_rows[g])
         nc.sync.dma_start(out=x_raw[0][:], in_=x_rows[0])
@@ -181,8 +182,11 @@ def tile_antisymmetricssprk2step_kernel(tc, h, x_bytes, x_scale, w, win, b, p, r
         def hq(g, gk):
             quant(hp_codes[g, gk][:], hp_scales[g, gk][:], hp_mix[g, gk][:].rearrange("p k t -> p (k t)"))
 
-        def hh(g):
-            nc.vector.tensor_scalar(out=h_nat[g][:], in0=h_nat[g][:], scalar1=0.5, scalar2=None, op0=ALU.mult)
+        def hh(eng, g):
+            if eng == "S":
+                nc.scalar.mul(h_nat[g][:], h_nat[g][:], 0.5)
+            else:
+                nc.vector.tensor_scalar(out=h_nat[g][:], in0=h_nat[g][:], scalar1=0.5, scalar2=None, op0=ALU.mult)
 
         def xc(eng, g):
             cp(eng, x_val[g][:], x_raw[g][:].bitcast(FP8))
@@ -210,18 +214,23 @@ def tile_antisymmetricssprk2step_kernel(tc, h, x_bytes, x_scale, w, win, b, p, r
         def wq(ng):
             quant(win_codes[ng][:], win_scales[ng][:], win_mix[ng][:].rearrange("p a m t -> p (a m t)"))
 
-        def drive(ps, g, ng, tn, codes, scales, lo, hi):
+        def drive_x(ps, g, ng, tn, lo, hi):
             c = slice(tn * P, (tn + 1) * P)
             k = slice(lo, hi)
             nc.tensor.matmul_mx(ps, lhsT=win_codes[ng][:, c].bitcast(FP8X4), lhsT_scale=win_scales[ng][:, c],
                                 rhs=x_codes[g][:, k].bitcast(FP8X4), rhs_scale=x_scales[g][:, k], start=True, stop=False)
+
+        def drive_a(ps, g, ng, tn, codes, scales, lo, hi):
+            c = slice(tn * P, (tn + 1) * P)
+            k = slice(lo, hi)
             for gk in range(G):
                 nc.tensor.matmul_mx(ps, lhsT=a_codes[gk, ng][:, c].bitcast(FP8X4), lhsT_scale=a_scales[gk, ng][:, c],
                                     rhs=codes[g, gk][:, k].bitcast(FP8X4), rhs_scale=scales[g, gk][:, k], start=False, stop=(gk == G - 1))
 
         def s(g, ng, tn):
             ps = bank["s", g, ng, tn] = psum.tile([P, N], F32, name="z", tag="bank", bufs=8)
-            drive(ps[:], g, ng, tn, hp_codes, hp_scales, 0, N)
+            drive_x(ps[:], g, ng, tn, 0, N)
+            drive_a(ps[:], g, ng, tn, hp_codes, hp_scales, 0, N)
 
         def S(g, ng, tn):
             nc.scalar.activation(v[g, ng][:, tn, :], bank["s", g, ng, tn][:], ACT.Tanh, bias=b_col[:, ng, tn:tn + 1])
@@ -254,10 +263,14 @@ def tile_antisymmetricssprk2step_kernel(tc, h, x_bytes, x_scale, w, win, b, p, r
         def vs(g, ng):
             nc.scalar.mul(v[g, ng][:], v[g, ng][:], 0.75)
 
-        def z(g, ng, tn, half, parts):
+        def zc(g, ng, tn, half, parts):
             n = N // parts
             ps = bank["z", g, ng, tn, half] = psum.tile([P, N], F32, name="z", tag="bank", bufs=8)
-            drive(ps[:, 0:n], g, ng, tn, u_codes, u_scales, n * half, n * (half + 1))
+            drive_x(ps[:, 0:n], g, ng, tn, n * half, n * (half + 1))
+
+        def z(g, ng, tn, half, parts):
+            n = N // parts
+            drive_a(bank["z", g, ng, tn, half][:, 0:n], g, ng, tn, u_codes, u_scales, n * half, n * (half + 1))
 
         def Z(g, ng, tn, half, parts):
             if (g, ng) not in e:
@@ -269,6 +282,11 @@ def tile_antisymmetricssprk2step_kernel(tc, h, x_bytes, x_scale, w, win, b, p, r
             n = N // parts
             k = slice(n * half, n * (half + 1))
             nc.vector.scalar_tensor_tensor(out=e[g, ng][:, tn, k], in0=v[g, ng][:, tn, k], scalar=0.75, in1=e[g, ng][:, tn, k], op0=ALU.mult, op1=ALU.add)
+
+        def ga(g, ng, tn, half, parts):
+            n = N // parts
+            k = slice(n * half, n * (half + 1))
+            nc.gpsimd.tensor_tensor(out=e[g, ng][:, tn, k], in0=e[g, ng][:, tn, k], in1=v[g, ng][:, tn, k], op=ALU.add)
 
         def o(g, ng, j):
             ps = bank["o", g, ng, j] = psum.tile([P, T, P], F32, name="o", tag="bank", bufs=8)
@@ -291,270 +309,284 @@ def tile_antisymmetricssprk2step_kernel(tc, h, x_bytes, x_scale, w, win, b, p, r
             nc.sync.dma_start(out=out_rows[g, :, lo:hi, N * ng:N * (ng + 1)], in_=o_tile[g, ng][:, lo:hi, :])
 
         step = dict(w=w, W=W, a=a, A=A, aq=aq, h_=h_, H_=H_, hg=hg, hq=hq, hh=hh, xc=xc, x_=x_, X_=X_, xq=xq, wl=wl, wq=wq,
-                    dm=dm, s=s, S=S, us=us, ug=ug, ul=ul, ui=ui, uq=uq, vs=vs, z=z, Z=Z, cb=cb, o=o, F=F, st=st)
+                    dm=dm, s=s, S=S, us=us, ug=ug, ul=ul, ui=ui, uq=uq, vs=vs, zc=zc, z=z, Z=Z, cb=cb, ga=ga, o=o, F=F, st=st)
         for line in PLAN:
             step[line[0]](*line[1:])
 
 
 PLAN = (
-    ("h_", 0, 0, 0),
-    ("H_", "S", 0, 0, 0),
     ("h_", 0, 1, 0),
+    ("h_", 0, 0, 0),
     ("H_", "V", 0, 1, 0),
     ("h_", 0, 0, 1),
-    ("H_", "S", 0, 0, 1),
+    ("H_", "S", 0, 0, 0),
     ("h_", 0, 1, 1),
-    ("H_", "S", 0, 1, 1),
-    ("hh", 0),
-    ("hg", 0, 1),
+    ("H_", "V", 0, 0, 1),
     ("dm", 2),
-    ("w", 0, 0, 0),
-    ("W", "V", 0, 0, 0),
-    ("w", 0, 0, 1),
-    ("W", "S", 0, 0, 1),
-    ("w", 0, 1, 0),
-    ("W", "S", 0, 1, 0),
-    ("a", 0, 0, 0),
-    ("A", "S", 0, 0, 0),
+    ("H_", "S", 0, 1, 1),
+    ("hh", "V", 0),
     ("w", 0, 1, 1),
-    ("W", "S", 0, 1, 1),
-    ("a", 0, 0, 1),
-    ("a", 0, 0, 2),
-    ("A", "S", 0, 0, 1),
-    ("A", "S", 0, 0, 2),
-    ("hg", 0, 0),
-    ("xc", "V", 0),
-    ("hq", 0, 0),
-    ("wl", "V", 1),
-    ("wq", 1),
+    ("hg", 0, 1),
+    ("w", 0, 1, 0),
+    ("w", 0, 0, 0),
+    ("W", "V", 0, 1, 1),
+    ("W", "S", 0, 1, 0),
     ("hq", 0, 1),
-    ("xc", "S", 1),
-    ("wl", "V", 0),
-    ("wq", 0),
-    ("x_", 0, 0),
-    ("X_", 0, 0),
-    ("x_", 0, 1),
-    ("a", 0, 0, 3),
-    ("A", "S", 0, 0, 3),
-    ("X_", 0, 1),
-    ("xq", 0),
-    ("a", 1, 0, 0),
-    ("A", "S", 1, 0, 0),
-    ("w", 1, 0, 0),
-    ("W", "S", 1, 0, 0),
-    ("w", 1, 0, 1),
-    ("W", "S", 1, 0, 1),
-    ("a", 1, 0, 1),
-    ("A", "S", 1, 0, 1),
+    ("W", "S", 0, 0, 0),
     ("a", 1, 0, 2),
-    ("A", "S", 1, 0, 2),
+    ("hg", 0, 0),
+    ("xc", "S", 0),
+    ("w", 1, 0, 0),
+    ("w", 1, 0, 1),
+    ("W", "V", 1, 0, 0),
     ("w", 1, 1, 0),
+    ("hq", 0, 0),
+    ("a", 1, 0, 1),
+    ("W", "S", 1, 0, 1),
+    ("wl", "V", 0),
+    ("a", 1, 0, 0),
     ("W", "S", 1, 1, 0),
     ("w", 1, 1, 1),
-    ("W", "V", 1, 1, 1),
+    ("A", "S", 1, 0, 0),
+    ("xc", "V", 1),
+    ("x_", 0, 0),
+    ("W", "S", 1, 1, 1),
+    ("w", 0, 0, 1),
+    ("A", "S", 1, 0, 1),
+    ("X_", 0, 0),
     ("a", 1, 0, 3),
-    ("A", "S", 1, 0, 3),
-    ("a", 0, 1, 0),
-    ("A", "S", 0, 1, 0),
-    ("h_", 1, 0, 0),
-    ("H_", "V", 1, 0, 0),
+    ("W", "S", 0, 0, 1),
+    ("x_", 0, 1),
+    ("A", "S", 1, 0, 2),
+    ("wq", 0),
     ("h_", 1, 1, 0),
-    ("H_", "S", 1, 1, 0),
-    ("a", 0, 1, 1),
-    ("A", "S", 0, 1, 1),
-    ("a", 0, 1, 2),
-    ("A", "S", 0, 1, 2),
-    ("aq", 0, 0),
-    ("aq", 1, 0),
-    ("x_", 1, 0),
-    ("X_", 1, 0),
-    ("x_", 1, 1),
-    ("X_", 1, 1),
-    ("xq", 1),
-    ("a", 0, 1, 3),
-    ("A", "S", 0, 1, 3),
-    ("aq", 0, 1),
-    ("a", 1, 1, 0),
-    ("A", "S", 1, 1, 0),
-    ("h_", 1, 0, 1),
-    ("H_", "S", 1, 0, 1),
-    ("hg", 1, 0),
-    ("hq", 1, 0),
+    ("A", "S", 1, 0, 3),
+    ("X_", 0, 1),
     ("h_", 1, 1, 1),
+    ("H_", "S", 1, 1, 0),
+    ("a", 0, 0, 1),
     ("H_", "S", 1, 1, 1),
+    ("aq", 1, 0),
+    ("a", 0, 0, 2),
+    ("wl", "S", 1),
+    ("xq", 0),
+    ("a", 0, 1, 0),
     ("hg", 1, 1),
-    ("a", 1, 1, 1),
-    ("A", "S", 1, 1, 1),
+    ("a", 0, 0, 0),
+    ("a", 1, 1, 0),
+    ("A", "V", 0, 0, 0),
     ("a", 1, 1, 2),
-    ("A", "S", 1, 1, 2),
+    ("A", "V", 1, 1, 0),
+    ("A", "S", 0, 0, 1),
     ("a", 1, 1, 3),
-    ("A", "S", 1, 1, 3),
-    ("aq", 1, 1),
-    ("s", 0, 0, 0),
-    ("S", 0, 0, 0),
-    ("s", 0, 0, 1),
-    ("S", 0, 0, 1),
-    ("us", 0, 0, 0),
-    ("s", 0, 0, 2),
-    ("S", 0, 0, 2),
+    ("wq", 1),
+    ("A", "S", 0, 0, 2),
+    ("a", 1, 1, 1),
     ("hq", 1, 1),
+    ("A", "S", 0, 1, 0),
+    ("a", 0, 0, 3),
+    ("A", "V", 1, 1, 1),
+    ("h_", 1, 0, 0),
+    ("A", "S", 0, 0, 3),
+    ("x_", 1, 0),
+    ("A", "S", 1, 1, 2),
+    ("aq", 0, 0),
+    ("x_", 1, 1),
+    ("A", "S", 1, 1, 3),
+    ("X_", 1, 0),
+    ("s", 0, 0, 0),
+    ("H_", "S", 1, 0, 0),
+    ("aq", 1, 1),
+    ("s", 0, 0, 1),
+    ("S", 0, 0, 0),
+    ("X_", 1, 1),
+    ("a", 0, 1, 1),
+    ("S", 0, 0, 1),
+    ("a", 0, 1, 2),
+    ("A", "S", 0, 1, 1),
+    ("us", 0, 0, 0),
+    ("a", 0, 1, 3),
+    ("A", "S", 0, 1, 2),
+    ("h_", 1, 0, 1),
+    ("A", "S", 0, 1, 3),
+    ("xq", 1),
     ("s", 0, 0, 3),
-    ("S", 0, 0, 3),
-    ("s", 0, 1, 0),
-    ("s", 0, 1, 1),
-    ("s", 0, 1, 2),
-    ("s", 0, 1, 3),
-    ("us", 0, 0, 1),
-    ("hh", 1),
-    ("ul", 0, 0, 0),
     ("ul", 0, 0, 1),
-    ("S", 0, 1, 0),
-    ("S", 0, 1, 1),
-    ("us", 0, 1, 0),
+    ("aq", 0, 1),
+    ("ul", 0, 0, 0),
+    ("hh", "V", 1),
+    ("s", 0, 0, 2),
+    ("H_", "S", 1, 0, 1),
+    ("s", 0, 1, 2),
+    ("S", 0, 0, 2),
+    ("hg", 1, 0),
+    ("S", 0, 0, 3),
+    ("s", 0, 1, 3),
     ("S", 0, 1, 2),
+    ("hq", 1, 0),
+    ("s", 0, 1, 1),
     ("S", 0, 1, 3),
+    ("us", 0, 0, 1),
+    ("s", 0, 1, 0),
+    ("S", 0, 1, 1),
     ("us", 0, 1, 1),
-    ("ul", 0, 0, 2),
-    ("ul", 0, 0, 3),
-    ("ui", 0, 0),
-    ("ug", 0, 1),
-    ("uq", 0, 0),
-    ("s", 1, 0, 0),
-    ("S", 1, 0, 0),
-    ("s", 1, 0, 1),
-    ("S", 1, 0, 1),
-    ("us", 1, 0, 0),
-    ("s", 1, 0, 2),
-    ("S", 1, 0, 2),
-    ("uq", 0, 1),
-    ("vs", 0, 0),
+    ("zc", 1, 0, 2, 0, 1),
+    ("S", 0, 1, 0),
+    ("zc", 0, 0, 1, 0, 1),
     ("s", 1, 0, 3),
+    ("ul", 0, 0, 3),
+    ("us", 0, 1, 0),
+    ("ul", 0, 0, 2),
+    ("s", 1, 0, 2),
     ("S", 1, 0, 3),
-    ("us", 1, 0, 1),
-    ("s", 1, 1, 0),
-    ("S", 1, 1, 0),
-    ("s", 1, 1, 1),
+    ("ui", 0, 0),
     ("s", 1, 1, 2),
+    ("vs", 0, 0),
+    ("s", 1, 0, 1),
+    ("ug", 0, 1),
+    ("s", 1, 1, 1),
+    ("S", 1, 0, 1),
+    ("zc", 0, 1, 3, 0, 1),
+    ("zc", 0, 0, 2, 0, 1),
+    ("S", 1, 0, 2),
+    ("s", 1, 1, 0),
     ("S", 1, 1, 1),
-    ("us", 1, 1, 0),
     ("s", 1, 1, 3),
+    ("S", 1, 1, 0),
+    ("us", 1, 0, 1),
+    ("vs", 0, 1),
+    ("zc", 0, 0, 0, 0, 1),
+    ("s", 1, 0, 0),
+    ("uq", 0, 0),
+    ("us", 1, 1, 0),
+    ("S", 1, 0, 0),
+    ("uq", 0, 1),
     ("S", 1, 1, 2),
-    ("S", 1, 1, 3),
-    ("us", 1, 1, 1),
-    ("ul", 1, 0, 0),
-    ("ul", 1, 0, 1),
-    ("ul", 1, 0, 2),
-    ("ul", 1, 0, 3),
-    ("ui", 1, 0),
-    ("uq", 1, 0),
-    ("ul", 1, 1, 0),
-    ("ul", 1, 1, 1),
-    ("ul", 1, 1, 2),
-    ("ul", 1, 1, 3),
-    ("ui", 1, 1),
-    ("uq", 1, 1),
+    ("zc", 0, 1, 1, 0, 1),
+    ("us", 1, 0, 0),
     ("z", 0, 0, 0, 0, 1),
+    ("S", 1, 1, 3),
+    ("zc", 0, 0, 3, 0, 1),
     ("Z", 0, 0, 0, 0, 1),
-    ("z", 0, 0, 1, 0, 1),
-    ("Z", 0, 0, 1, 0, 1),
-    ("z", 0, 0, 2, 0, 1),
-    ("Z", 0, 0, 2, 0, 1),
     ("z", 0, 0, 3, 0, 1),
-    ("Z", 0, 0, 3, 0, 1),
-    ("z", 0, 1, 0, 0, 1),
-    ("Z", 0, 1, 0, 0, 1),
-    ("cb", 0, 1, 0, 0, 1),
+    ("us", 1, 1, 1),
     ("z", 0, 1, 1, 0, 1),
+    ("Z", 0, 0, 3, 0, 1),
+    ("z", 0, 0, 1, 0, 1),
+    ("ug", 1, 0),
     ("Z", 0, 1, 1, 0, 1),
-    ("cb", 0, 1, 1, 0, 1),
+    ("z", 0, 0, 2, 0, 1),
+    ("Z", 0, 0, 1, 0, 1),
+    ("ga", 0, 1, 1, 0, 1),
+    ("zc", 1, 1, 0, 1, 2),
+    ("Z", 0, 0, 2, 0, 1),
+    ("zc", 0, 1, 2, 0, 1),
     ("z", 0, 1, 2, 0, 1),
-    ("Z", 0, 1, 2, 0, 1),
-    ("cb", 0, 1, 2, 0, 1),
     ("z", 0, 1, 3, 0, 1),
+    ("Z", 0, 1, 2, 0, 1),
+    ("zc", 0, 1, 0, 0, 1),
     ("Z", 0, 1, 3, 0, 1),
-    ("cb", 0, 1, 3, 0, 1),
-    ("o", 0, 0, 0),
-    ("F", 0, 0, 0),
-    ("st", 0, 0, 0, 1),
-    ("o", 0, 0, 1),
-    ("F", 0, 0, 1),
-    ("st", 0, 0, 1, 2),
-    ("z", 1, 0, 0, 0, 1),
-    ("Z", 1, 0, 0, 0, 1),
-    ("cb", 1, 0, 0, 0, 1),
-    ("z", 1, 0, 1, 0, 1),
-    ("Z", 1, 0, 1, 0, 1),
-    ("cb", 1, 0, 1, 0, 1),
-    ("o", 0, 0, 2),
-    ("F", 0, 0, 2),
-    ("st", 0, 0, 2, 3),
+    ("ug", 1, 1),
+    ("zc", 1, 1, 0, 0, 2),
+    ("ga", 0, 1, 2, 0, 1),
     ("o", 0, 0, 3),
+    ("vs", 1, 0),
+    ("o", 0, 0, 1),
+    ("ga", 0, 1, 3, 0, 1),
+    ("z", 0, 1, 0, 0, 1),
+    ("zc", 1, 0, 1, 0, 1),
+    ("o", 0, 0, 0),
+    ("Z", 0, 1, 0, 0, 1),
+    ("uq", 1, 0),
+    ("ga", 0, 1, 0, 0, 1),
+    ("zc", 1, 0, 0, 0, 1),
+    ("uq", 1, 1),
     ("F", 0, 0, 3),
+    ("z", 1, 0, 1, 0, 1),
+    ("F", 0, 0, 0),
+    ("z", 1, 0, 0, 0, 1),
     ("st", 0, 0, 3, 4),
-    ("z", 1, 0, 2, 0, 1),
-    ("Z", 1, 0, 2, 0, 1),
-    ("cb", 1, 0, 2, 0, 1),
-    ("z", 1, 0, 3, 0, 1),
-    ("o", 0, 1, 0),
-    ("o", 0, 1, 1),
-    ("F", 0, 1, 0),
-    ("F", 0, 1, 1),
-    ("Z", 1, 0, 3, 0, 1),
-    ("cb", 1, 0, 3, 0, 1),
-    ("st", 0, 1, 0, 1),
-    ("st", 0, 1, 1, 2),
-    ("z", 1, 1, 0, 0, 2),
-    ("Z", 1, 1, 0, 0, 2),
-    ("cb", 1, 1, 0, 0, 2),
+    ("Z", 1, 0, 1, 0, 1),
+    ("F", 0, 0, 1),
+    ("zc", 1, 1, 2, 0, 2),
+    ("st", 0, 0, 0, 1),
+    ("zc", 1, 1, 1, 0, 2),
+    ("Z", 1, 0, 0, 0, 1),
     ("z", 1, 1, 1, 0, 2),
+    ("ga", 1, 0, 1, 0, 1),
+    ("zc", 1, 1, 2, 1, 2),
+    ("st", 0, 0, 1, 2),
+    ("zc", 1, 1, 3, 0, 2),
     ("Z", 1, 1, 1, 0, 2),
-    ("cb", 1, 1, 1, 0, 2),
     ("z", 1, 1, 2, 0, 2),
+    ("z", 1, 1, 0, 0, 2),
+    ("cb", 1, 1, 1, 0, 2),
     ("Z", 1, 1, 2, 0, 2),
-    ("cb", 1, 1, 2, 0, 2),
     ("z", 1, 1, 3, 0, 2),
-    ("o", 0, 1, 2),
-    ("o", 0, 1, 3),
-    ("F", 0, 1, 2),
-    ("F", 0, 1, 3),
-    ("o", 1, 0, 0),
-    ("o", 1, 0, 1),
-    ("Z", 1, 1, 3, 0, 2),
-    ("cb", 1, 1, 3, 0, 2),
-    ("st", 0, 1, 2, 3),
-    ("st", 0, 1, 3, 4),
-    ("F", 1, 0, 0),
-    ("st", 1, 0, 0, 1),
-    ("F", 1, 0, 1),
-    ("st", 1, 0, 1, 2),
-    ("z", 1, 1, 0, 1, 2),
-    ("Z", 1, 1, 0, 1, 2),
-    ("cb", 1, 1, 0, 1, 2),
-    ("z", 1, 1, 1, 1, 2),
-    ("Z", 1, 1, 1, 1, 2),
-    ("cb", 1, 1, 1, 1, 2),
+    ("ga", 1, 0, 0, 0, 1),
+    ("Z", 1, 1, 0, 0, 2),
+    ("zc", 1, 1, 3, 1, 2),
+    ("cb", 1, 1, 2, 0, 2),
     ("z", 1, 1, 2, 1, 2),
+    ("Z", 1, 1, 3, 0, 2),
+    ("cb", 1, 1, 0, 0, 2),
+    ("zc", 1, 1, 1, 1, 2),
     ("Z", 1, 1, 2, 1, 2),
+    ("z", 1, 1, 0, 1, 2),
+    ("cb", 1, 1, 3, 0, 2),
+    ("z", 1, 1, 1, 1, 2),
+    ("Z", 1, 1, 0, 1, 2),
     ("cb", 1, 1, 2, 1, 2),
-    ("z", 1, 1, 3, 1, 2),
-    ("o", 1, 0, 2),
-    ("o", 1, 0, 3),
-    ("o", 1, 1, 0),
+    ("o", 0, 1, 0),
+    ("Z", 1, 1, 1, 1, 2),
+    ("cb", 1, 1, 0, 1, 2),
+    ("o", 0, 1, 3),
+    ("F", 0, 1, 0),
+    ("o", 0, 1, 1),
     ("o", 1, 1, 1),
-    ("Z", 1, 1, 3, 1, 2),
-    ("cb", 1, 1, 3, 1, 2),
-    ("o", 1, 1, 2),
-    ("o", 1, 1, 3),
-    ("F", 1, 0, 2),
-    ("st", 1, 0, 2, 3),
-    ("F", 1, 0, 3),
-    ("st", 1, 0, 3, 4),
-    ("F", 1, 1, 0),
-    ("st", 1, 1, 0, 1),
+    ("F", 0, 1, 3),
+    ("st", 0, 1, 0, 1),
+    ("o", 0, 1, 2),
+    ("z", 1, 0, 2, 0, 1),
+    ("F", 0, 1, 1),
+    ("st", 0, 1, 3, 4),
+    ("zc", 1, 0, 3, 0, 1),
+    ("F", 0, 1, 2),
+    ("Z", 1, 0, 2, 0, 1),
+    ("st", 0, 1, 1, 2),
+    ("z", 1, 1, 3, 1, 2),
+    ("z", 1, 0, 3, 0, 1),
     ("F", 1, 1, 1),
+    ("Z", 1, 1, 3, 1, 2),
+    ("st", 0, 1, 2, 3),
+    ("ga", 1, 0, 2, 0, 1),
+    ("o", 1, 1, 0),
+    ("cb", 1, 1, 3, 1, 2),
+    ("Z", 1, 0, 3, 0, 1),
     ("st", 1, 1, 1, 2),
-    ("F", 1, 1, 2),
-    ("st", 1, 1, 2, 3),
+    ("cb", 1, 1, 1, 1, 2),
+    ("F", 1, 1, 0),
+    ("ga", 1, 0, 3, 0, 1),
+    ("o", 1, 1, 3),
+    ("o", 1, 1, 2),
     ("F", 1, 1, 3),
+    ("st", 1, 1, 0, 1),
+    ("o", 0, 0, 2),
+    ("F", 1, 1, 2),
     ("st", 1, 1, 3, 4),
+    ("o", 1, 0, 3),
+    ("F", 0, 0, 2),
+    ("st", 1, 1, 2, 3),
+    ("o", 1, 0, 1),
+    ("F", 1, 0, 3),
+    ("st", 0, 0, 2, 3),
+    ("o", 1, 0, 2),
+    ("F", 1, 0, 1),
+    ("st", 1, 0, 3, 4),
+    ("o", 1, 0, 0),
+    ("F", 1, 0, 2),
+    ("st", 1, 0, 1, 2),
+    ("F", 1, 0, 0),
+    ("st", 1, 0, 2, 3),
+    ("st", 1, 0, 0, 1),
 )

@@ -16,9 +16,15 @@ B, D, X = 1024, 1024, 512
 P = 128
 T = 4
 N = P * T
-G = D // N
-H = B // N
-ACC = ((0, 0),)
+HALVES = B // N
+GROUPS = D // N
+
+BANKS = 8
+PAGES = 7
+MIXES = 12
+
+SUM_ON_TENSOR = (1, 0)
+
 FLOPS = 2 * B * D * (X + 2 * D)
 
 
@@ -26,567 +32,380 @@ def tile_antisymmetricssprk2step_kernel(tc, h, x_bytes, x_scale, w, win, b, p, r
     nc = tc.nc
     with ExitStack() as ctx:
         keep = ctx.enter_context(tc.tile_pool(name="keep", bufs=1))
-        work = ctx.enter_context(tc.tile_pool(name="work", bufs=2))
-        psum = ctx.enter_context(tc.psum_pool(name="psum", bufs=4))
+        work = ctx.enter_context(tc.tile_pool(name="work", bufs=1))
+        psum = ctx.enter_context(tc.psum_pool(name="psum", bufs=BANKS))
         ctx.enter_context(tc.manual_schedule())
 
-        def kt(name, shape, dtype, align=64):
-            return keep.tile(shape, dtype, name=name, align_bytes=align)
+        def kept(name, shape, dtype):
+            return keep.tile(shape, dtype, name=name, align_bytes=64)
+
+        def kept_grid(name, shape, dtype):
+            return {(i, j): kept("%s_%d%d" % (name, i, j), shape, dtype) for i in range(2) for j in range(2)}
 
         def page(name, shape, dtype):
-            return work.tile(shape, dtype, name=name, tag="page", bufs=7, align_bytes=64)
+            return work.tile(shape, dtype, name=name, tag="page", bufs=PAGES, align_bytes=64)
 
         def mix(name, shape):
-            return work.tile(shape, BF16, name=name, tag="mix", bufs=12, align_bytes=64)
+            return work.tile(shape, BF16, name=name, tag="mix", bufs=MIXES, align_bytes=64)
 
-        def grid(name, shape, dtype, na, nb):
-            return {(i, j): kt("%s%d%d" % (name, i, j), shape, dtype) for i in range(na) for j in range(nb)}
+        def bank(shape):
+            return psum.tile(shape, F32, name="bank")
 
-        u_codes = grid("u_codes", [P, N], U32, H, G)
-        u_scales = grid("u_scales", [P, N], U8, H, G)
-        warm_codes = u_codes[1, 1]
-        warm_scales = u_scales[1, 1]
-        nc.vector.memset(warm_codes[:], 0)
-        nc.vector.memset(warm_scales[:].bitcast(U32), 0)
-        r_col = kt("r_col", [P, G, T], BF16)
-        p_col = kt("p_col", [P, G, T], BF16)
-        b_col = kt("b_col", [P, G, T], BF16)
-        s_col = kt("s_col", [P, T], F32)
-        nc.scalar.dma_start(out=r_col[:], in_=r.rearrange("(g p t) -> p g t", p=P, t=T))
-        nc.scalar.dma_start(out=p_col[:], in_=p.rearrange("(g p t) -> p g t", p=P, t=T))
-        nc.scalar.dma_start(out=s_col[:], in_=x_scale.rearrange("o (p t) -> p (o t)", p=P, t=T))
-        nc.scalar.dma_start(out=b_col[:], in_=b.rearrange("(g p t) -> p g t", p=P, t=T))
-
-        w_rows = w.rearrange("(g p t) c -> g p t c", p=P, t=T)
         h_rows = h.rearrange("(g p t) c -> g p t c", p=P, t=T)
+        w_rows = w.rearrange("(g p t) c -> g p t c", p=P, t=T)
         x_rows = x_bytes.rearrange("(g p t) c -> g p t c", p=P, t=T)
         out_rows = out.rearrange("(g p t) c -> g p t c", p=P, t=T)
-        w_nat = [page("w_nat%d" % g, [P, T, D], BF16) for g in range(G)]
-        h_nat = [kt("h_nat%d" % g, [P, T, D], BF16) for g in range(H)]
-        x_raw = [kt("x_raw%d" % g, [P, T, X], U8) for g in range(H)]
+        h_nat = [kept("h_nat_%d" % g, [P, T, D], BF16) for g in range(HALVES)]
+        w_nat = [page("w_nat_%d" % g, [P, T, D], BF16) for g in range(GROUPS)]
         win_nat = page("win_nat", [P, T, D], BF16)
-        nc.sync.dma_start(out=h_nat[0][:, 0:1, :], in_=h_rows[0, :, 0:1, :])
-        nc.sync.dma_start(out=h_nat[0][:, 1:2, :], in_=h_rows[0, :, 1:2, :])
-        nc.sync.dma_start(out=h_nat[0][:, 2:4, :], in_=h_rows[0, :, 2:4, :])
-        for g in range(G):
+        x_raw = [kept("x_raw_%d" % g, [P, T, X], U8) for g in range(HALVES)]
+
+        r_col = kept("r_col", [P, GROUPS, T], BF16)
+        p_col = kept("p_col", [P, GROUPS, T], BF16)
+        b_col = kept("b_col", [P, GROUPS, T], BF16)
+        s_col = kept("s_col", [P, T], F32)
+        for col, vec in ((r_col, r), (p_col, p), (b_col, b)):
+            nc.scalar.dma_start(out=col[:], in_=vec.rearrange("(g p t) -> p g t", p=P, t=T))
+        nc.scalar.dma_start(out=s_col[:], in_=x_scale.rearrange("o (p t) -> p (o t)", p=P, t=T))
+
+        for lo, hi in ((0, 1), (1, 2), (2, 4)):
+            nc.sync.dma_start(out=h_nat[0][:, lo:hi, :], in_=h_rows[0, :, lo:hi, :])
+        for g in range(GROUPS):
             nc.sync.dma_start(out=w_nat[g][:], in_=w_rows[g])
         nc.sync.dma_start(out=x_raw[0][:], in_=x_rows[0])
         nc.sync.dma_start(out=win_nat[:], in_=win.rearrange("(p t) c -> p t c", p=P, t=T))
         nc.sync.dma_start(out=x_raw[1][:], in_=x_rows[1])
         nc.sync.dma_start(out=h_nat[1][:], in_=h_rows[1])
 
-        ident = kt("ident", [P, P], F32)
-        ident_b = kt("ident_b", [P, P], BF16)
+        a_codes = kept_grid("a_codes", [P, N], U32)
+        a_scales = kept_grid("a_scales", [P, N], U8)
+        hp_codes = kept_grid("hp_codes", [P, N], U32)
+        hp_scales = kept_grid("hp_scales", [P, N], U8)
+        u_codes = kept_grid("u_codes", [P, N], U32)
+        u_scales = kept_grid("u_scales", [P, N], U8)
+        x_codes = [kept("x_codes_%d" % g, [P, N], U32) for g in range(HALVES)]
+        x_scales = [kept("x_scales_%d" % g, [P, N], U8) for g in range(HALVES)]
+        win_codes = [kept("win_codes_%d" % g, [P, N], U32) for g in range(GROUPS)]
+        win_scales = [kept("win_scales_%d" % g, [P, N], U8) for g in range(GROUPS)]
+        x_val = [kept("x_val_%d" % g, [P, T, X], BF16) for g in range(HALVES)]
+        h_turned = kept_grid("h_turned", [P, N, T], BF16)
+        v = kept_grid("v", [P, T, N], F32)
+        w_turned, a_mix, hp_mix, x_mix, win_mix, u_line, u_mix, t2, rows, banks = ({} for i in range(10))
+
+        zero_codes, zero_scales = u_codes[1, 1], u_scales[1, 1]
+        nc.vector.memset(zero_codes[:], 0)
+        nc.vector.memset(zero_scales[:].bitcast(U32), 0)
+        ident = kept("ident", [P, P], F32)
         make_identity(nc, ident[:])
-        warm = kt("warm", [P, 1], F32)
-        nc.vector.memset(warm[:], 0.0)
-        nc.scalar.activation(warm[:], warm[:], ACT.Tanh)
-        dg = kt("dg", [P, G * T, P], BF16)
-        dn = kt("dn", [P, G * T, P], BF16)
-        nc.vector.tensor_copy(ident_b[:], ident[:])
+        table = kept("table", [P, 1], F32)
+        nc.vector.memset(table[:], 0.0)
+        nc.scalar.activation(table[:], table[:], ACT.Tanh)
+        ident_bf = kept("ident_bf", [P, P], BF16)
+        nc.vector.tensor_copy(ident_bf[:], ident[:])
+        diag = kept("diag", [P, GROUPS * T, P], BF16)
+        minus = kept("minus", [P, GROUPS * T, P], BF16)
         nc.vector.tensor_tensor(
-            out=dg[:],
-            in0=ident_b[:].unsqueeze(1).to_broadcast([P, G * T, P]),
-            in1=r_col[:].rearrange("p g t -> p (g t)").unsqueeze(2).to_broadcast([P, G * T, P]),
+            out=diag[:],
+            in0=ident_bf[:].unsqueeze(1).to_broadcast([P, GROUPS * T, P]),
+            in1=r_col[:].rearrange("p g t -> p (g t)").unsqueeze(2).to_broadcast([P, GROUPS * T, P]),
             op=ALU.mult,
         )
-        nc.vector.tensor_scalar(out=dn[:], in0=dg[:], scalar1=-1.0, scalar2=None, op0=ALU.mult)
-        ph_col = kt("ph_col", [P, G, T], BF16)
-        nc.vector.tensor_scalar(out=ph_col[:], in0=p_col[:], scalar1=0.5, scalar2=None, op0=ALU.mult)
+        nc.vector.tensor_scalar(out=minus[:], in0=diag[:], scalar1=-1.0, scalar2=None, op0=ALU.mult)
+        half_p = kept("half_p", [P, GROUPS, T], F32)
+        nc.vector.tensor_scalar(out=half_p[:], in0=p_col[:], scalar1=0.5, scalar2=None, op0=ALU.mult)
 
-        ph_f32 = kt("ph_f32", [P, G, T], F32)
-        nc.vector.tensor_scalar(out=ph_f32[:], in0=p_col[:], scalar1=0.5, scalar2=None, op0=ALU.mult)
+        def quantise(codes, scales, in_):
+            nc.vector.quantize_mx(out=codes[:].bitcast(FP8X4), scales=scales[:], in_=in_)
 
-        def cp(eng, dst, src):
-            if eng == "S":
-                nc.scalar.copy(dst, src)
-            else:
-                nc.vector.tensor_copy(dst, src)
+        def words(tile, t):
+            return tile[:, t, :].bitcast(F32)
 
-        def quant(codes, scales, in_):
-            nc.vector.quantize_mx(out=codes.bitcast(FP8X4), scales=scales, in_=in_)
+        def turn(dst, tile, t, contraction_pass, u):
+            first = contraction_pass * N // 2
+            nc.tensor.transpose(dst, words(tile, t)[:, first + u:first + N // 2:2], ident[:])
 
-        wt = {}
-        a_codes = grid("a_codes", [P, N], U32, G, G)
-        a_scales = grid("a_scales", [P, N], U8, G, G)
-        hT = grid("hT", [P, N, T], BF16, H, G)
-        hp_codes = grid("hp_codes", [P, N], U32, H, G)
-        hp_scales = grid("hp_scales", [P, N], U8, H, G)
-        x_val = [kt("x_val%d" % g, [P, T, X], BF16) for g in range(H)]
-        x_codes = [kt("x_codes%d" % g, [P, N], U32) for g in range(H)]
-        x_scales = [kt("x_scales%d" % g, [P, N], U8) for g in range(H)]
-        win_codes = [kt("win_codes%d" % g, [P, N], U32) for g in range(G)]
-        win_scales = [kt("win_scales%d" % g, [P, N], U8) for g in range(G)]
-        v = grid("v", [P, T, N], F32, H, G)
-        bank = {}
-        a_mix = {}
-        hp_mix = {}
-        x_mix = {}
-        win_mix = {}
-        u_mix = {}
-        e = {}
-        o_tile = {}
+        def multiply(dst, lhs, lhs_scale, cols, rhs, rhs_scale, start, stop):
+            nc.tensor.matmul_mx(
+                dst, lhsT=lhs[:, cols].bitcast(FP8X4), lhsT_scale=lhs_scale[:, cols],
+                rhs=rhs[:].bitcast(FP8X4), rhs_scale=rhs_scale[:], start=start, stop=stop)
 
+        def drive(key, half, group, t, codes, scales):
+            acc = banks[key] = bank([P, N])
+            cols = slice(P * t, P * (t + 1))
+            multiply(acc[:], win_codes[group], win_scales[group], cols, x_codes[half], x_scales[half], True, False)
+            for k in range(GROUPS):
+                multiply(acc[:], a_codes[k, group], a_scales[k, group], cols, codes[half, k], scales[half, k],
+                         False, k == GROUPS - 1)
 
-        def dm(passes):
-            ps = psum.tile([P, N], F32, name="z", tag="bank", bufs=8)
+        def warm(passes):
+            dst = bank([P, N])
             for i in range(passes):
-                nc.tensor.matmul_mx(ps[:], lhsT=warm_codes[:, 0:P].bitcast(FP8X4), lhsT_scale=warm_scales[:, 0:P],
-                                    rhs=warm_codes[:].bitcast(FP8X4), rhs_scale=warm_scales[:], start=True, stop=True)
+                multiply(dst[:], zero_codes, zero_scales, slice(0, P), zero_codes, zero_scales, True, True)
 
-        dm(7)
-
-        def words_turn(key, words, lo, pair):
-            ps = bank[key] = psum.tile([P, 2, 2, P], F32, name="o", tag="bank", bufs=8)
-            for tt in range(2):
-                for u in range(2):
-                    nc.tensor.transpose(ps[:, u, tt, :], words[:, 2 * pair + tt, lo + u:lo + 256:2], ident[:])
-
-        def w(ng, gk, u):
-            ps = bank["w", ng, gk, u] = psum.tile([P, T, P], F32, name="o", tag="bank", bufs=8)
-            for tn in range(T):
-                nc.tensor.transpose(ps[:, tn, :], w_nat[ng][:, tn, :].bitcast(F32)[:, 256 * gk + u:256 * (gk + 1):2], ident[:])
-
-        def W(eng, ng, gk, u):
-            if (gk, ng) not in wt:
-                wt[gk, ng] = mix("wt", [P, 2, N, 2])
-            dst = wt[gk, ng][:, u, :, :].rearrange("p n e -> p (n e)").bitcast(F32)
-            cp(eng, dst.rearrange("p (m t) -> p m t", t=T), bank["w", ng, gk, u][:].rearrange("p t m -> p m t"))
-
-        def a(gk, ng, q):
-            ps = bank["a", gk, ng, q] = psum.tile([P, T, P], F32, name="z", tag="bank", bufs=8)
+        def turn_w(n, k, u):
+            dst = banks["w", n, k, u] = bank([P, T, P])
             for t in range(T):
-                nc.tensor.matmul(ps[:, t, :], dg[:, gk * T + t, :], w_nat[gk][:, t, N * ng + P * q:N * ng + P * (q + 1)], start=True, stop=False)
-                nc.tensor.matmul(ps[:, t, :], dn[:, gk * T + t, :], wt[gk, ng][:, t // 2, P * q:P * (q + 1), t % 2], start=False, stop=True)
+                turn(dst[:, t, :], w_nat[n], t, k, u)
 
-        def A(eng, gk, ng, q):
-            if (gk, ng) not in a_mix:
-                a_mix[gk, ng] = mix("a_mix", [P, T, P, T])
+        def copy_w(copy, n, k, u):
+            if (k, n) not in w_turned:
+                w_turned[k, n] = mix("w_turned", [P, 2, N, 2])
+            dst = w_turned[k, n][:, u, :, :].rearrange("p n e -> p (n e)").bitcast(F32)
+            copy(dst.rearrange("p (m t) -> p m t", t=T), banks["w", n, k, u][:].rearrange("p t m -> p m t"))
+
+        def build_a(k, n, q):
+            acc = banks["a", k, n, q] = bank([P, T, P])
+            cols = slice(P * q, P * (q + 1))
+            for t in range(T):
+                nc.tensor.matmul(acc[:, t, :], diag[:, k * T + t, :], w_nat[k][:, t, N * n + P * q:N * n + P * (q + 1)],
+                                 start=True, stop=False)
+                nc.tensor.matmul(acc[:, t, :], minus[:, k * T + t, :], w_turned[k, n][:, t // 2, cols, t % 2],
+                                 start=False, stop=True)
+
+        def copy_a(copy, k, n, q):
+            if (k, n) not in a_mix:
+                a_mix[k, n] = mix("a_mix", [P, T, P, T])
             m = P // T
-            cp(eng, a_mix[gk, ng][:, :, m * q:m * (q + 1), :], bank["a", gk, ng, q][:].rearrange("p t (m a) -> p a m t", a=T))
+            copy(a_mix[k, n][:, :, m * q:m * (q + 1), :], banks["a", k, n, q][:].rearrange("p t (m i) -> p i m t", i=T))
 
-        def aq(gk, ng):
-            quant(a_codes[gk, ng][:], a_scales[gk, ng][:], a_mix[gk, ng][:].rearrange("p a m t -> p (a m t)"))
+        def quantise_a(k, n):
+            quantise(a_codes[k, n], a_scales[k, n], a_mix[k, n][:].rearrange("p i m t -> p (i m t)"))
 
-        def h_(g, gk, pair):
-            words_turn(("h", g, gk, pair), h_nat[g][:].bitcast(F32), 256 * gk, pair)
+        def turn_h(g, pair, k):
+            dst = banks["h", g, pair, k] = bank([P, 2, 2, P])
+            for j in range(2):
+                for u in range(2):
+                    turn(dst[:, u, j, :], h_nat[g], 2 * pair + j, k, u)
 
-        def H_(eng, g, gk, pair):
-            dst = hT[g, gk][:, 256 * pair:256 * (pair + 1), :].rearrange("p k t -> p (k t)").bitcast(F32)
-            cp(eng, dst.rearrange("p (k u) -> p k u", u=2), bank["h", g, gk, pair][:].rearrange("p u t m -> p (t m) u"))
+        def copy_h(copy, g, pair, k):
+            dst = h_turned[g, k][:, 2 * P * pair:2 * P * (pair + 1), :].rearrange("p c t -> p (c t)").bitcast(F32)
+            copy(dst.rearrange("p (c u) -> p c u", u=2), banks["h", g, pair, k][:].rearrange("p u j i -> p (j i) u"))
 
-        def hg(g, gk):
-            hp_mix[g, gk] = mix("hp_mix", [P, N, T])
-            nc.vector.tensor_tensor(out=hp_mix[g, gk][:], in0=hT[g, gk][:], in1=p_col[:, gk, :].unsqueeze(1).to_broadcast([P, N, T]), op=ALU.mult)
+        def gain_h(g, k):
+            hp_mix[g, k] = mix("hp_mix", [P, N, T])
+            nc.vector.tensor_tensor(out=hp_mix[g, k][:], in0=h_turned[g, k][:],
+                                    in1=p_col[:, k, :].unsqueeze(1).to_broadcast([P, N, T]), op=ALU.mult)
 
-        def hq(g, gk):
-            quant(hp_codes[g, gk][:], hp_scales[g, gk][:], hp_mix[g, gk][:].rearrange("p k t -> p (k t)"))
+        def quantise_h(g, k):
+            quantise(hp_codes[g, k], hp_scales[g, k], hp_mix[g, k][:].rearrange("p c t -> p (c t)"))
 
-        def hh(eng, g):
-            if eng == "S":
-                nc.scalar.mul(h_nat[g][:], h_nat[g][:], 0.5)
-            else:
-                nc.vector.tensor_scalar(out=h_nat[g][:], in0=h_nat[g][:], scalar1=0.5, scalar2=None, op0=ALU.mult)
+        def halve_h(g):
+            nc.vector.tensor_scalar(out=h_nat[g][:], in0=h_nat[g][:], scalar1=0.5, scalar2=None, op0=ALU.mult)
 
-        def xc(eng, g):
-            cp(eng, x_val[g][:], x_raw[g][:].bitcast(FP8))
+        def widen_x(copy, g):
+            copy(x_val[g][:], x_raw[g][:].bitcast(FP8))
 
-        def x_(g, pair):
-            words_turn(("x", g, pair), x_val[g][:].bitcast(F32), 0, pair)
+        def turn_x(g, pair):
+            dst = banks["x", g, pair] = bank([P, 2, 2, P])
+            for j in range(2):
+                for u in range(2):
+                    turn(dst[:, u, j, :], x_val[g], 2 * pair + j, 0, u)
 
-        def X_(g, pair):
+        def scale_x(g, pair):
             if g not in x_mix:
-                x_mix[g] = mix("hp_mix", [P, N, T])
+                x_mix[g] = mix("x_mix", [P, N, T])
+            turned = banks["x", g, pair][:].rearrange("p u j i -> p u (j i)").bitcast(BF16)
             nc.vector.tensor_tensor(
-                out=x_mix[g][:, 256 * pair:256 * (pair + 1), :].rearrange("p k (u e) -> p k u e", e=2),
-                in0=bank["x", g, pair][:].rearrange("p u t m -> p u (t m)").bitcast(BF16).rearrange("p u (k e) -> p k u e", e=2),
-                in1=s_col[:].rearrange("p (u e) -> p u e", e=2).unsqueeze(1).to_broadcast([P, 256, 2, 2]),
+                out=x_mix[g][:, 2 * P * pair:2 * P * (pair + 1), :].rearrange("p c (u e) -> p c u e", e=2),
+                in0=turned.rearrange("p u (c e) -> p c u e", e=2),
+                in1=s_col[:].rearrange("p (u e) -> p u e", e=2).unsqueeze(1).to_broadcast([P, 2 * P, 2, 2]),
                 op=ALU.mult,
             )
 
-        def xq(g):
-            quant(x_codes[g][:], x_scales[g][:], x_mix[g][:].rearrange("p k t -> p (k t)"))
+        def quantise_x(g):
+            quantise(x_codes[g], x_scales[g], x_mix[g][:].rearrange("p c t -> p (c t)"))
 
-        def wl(eng, ng):
-            win_mix[ng] = mix("win_mix", [P, T, P, T])
-            cp(eng, win_mix[ng][:], win_nat[:, :, N * ng:N * (ng + 1)].rearrange("p t (m a) -> p a m t", a=T))
+        def lay_win(copy, n):
+            win_mix[n] = mix("win_mix", [P, T, P, T])
+            copy(win_mix[n][:], win_nat[:, :, N * n:N * (n + 1)].rearrange("p t (m i) -> p i m t", i=T))
 
-        def wq(ng):
-            quant(win_codes[ng][:], win_scales[ng][:], win_mix[ng][:].rearrange("p a m t -> p (a m t)"))
+        def quantise_win(n):
+            quantise(win_codes[n], win_scales[n], win_mix[n][:].rearrange("p i m t -> p (i m t)"))
 
-        def drive_x(ps, g, ng, tn, lo, hi):
-            c = slice(tn * P, (tn + 1) * P)
-            k = slice(lo, hi)
-            nc.tensor.matmul_mx(ps, lhsT=win_codes[ng][:, c].bitcast(FP8X4), lhsT_scale=win_scales[ng][:, c],
-                                rhs=x_codes[g][:, k].bitcast(FP8X4), rhs_scale=x_scales[g][:, k], start=True, stop=False)
+        def drive_1(g, n, t):
+            drive(("z1", g, n, t), g, n, t, hp_codes, hp_scales)
 
-        def drive_a(ps, g, ng, tn, codes, scales, lo, hi):
-            c = slice(tn * P, (tn + 1) * P)
-            k = slice(lo, hi)
-            for gk in range(G):
-                nc.tensor.matmul_mx(ps, lhsT=a_codes[gk, ng][:, c].bitcast(FP8X4), lhsT_scale=a_scales[gk, ng][:, c],
-                                    rhs=codes[g, gk][:, k].bitcast(FP8X4), rhs_scale=scales[g, gk][:, k], start=False, stop=(gk == G - 1))
+        def tanh_1(g, n, t):
+            nc.scalar.activation(v[g, n][:, t, :], banks["z1", g, n, t][:], ACT.Tanh, bias=b_col[:, n, t:t + 1])
 
-        def s(g, ng, tn):
-            ps = bank["s", g, ng, tn] = psum.tile([P, N], F32, name="z", tag="bank", bufs=8)
-            drive_x(ps[:], g, ng, tn, 0, N)
-            drive_a(ps[:], g, ng, tn, hp_codes, hp_scales, 0, N)
-
-        def S(g, ng, tn):
-            nc.scalar.activation(v[g, ng][:, tn, :], bank["s", g, ng, tn][:], ACT.Tanh, bias=b_col[:, ng, tn:tn + 1])
-
-        def us(g, ng, half):
-            c = slice(2 * half, 2 * half + 2)
+        def state(g, n, s):
+            ts = slice(2 * s, 2 * s + 2)
             nc.vector.scalar_tensor_tensor(
-                out=v[g, ng][:, c, :], in0=hT[g, ng][:, :, c].rearrange("p k t -> p t k"), scalar=1.5,
-                in1=v[g, ng][:, c, :], op0=ALU.mult, op1=ALU.add)
+                out=v[g, n][:, ts, :], in0=h_turned[g, n][:, :, ts].rearrange("p c t -> p t c"), scalar=1.5,
+                in1=v[g, n][:, ts, :], op0=ALU.mult, op1=ALU.add)
 
-        def ug(g, ng):
-            u_mix[g, ng] = mix("u_mix", [P, N, T])
-            nc.vector.tensor_tensor(out=u_mix[g, ng][:], in0=v[g, ng][:].rearrange("p t k -> p k t"),
-                                    in1=ph_col[:, ng, :].unsqueeze(1).to_broadcast([P, N, T]), op=ALU.mult)
+        def gain_u(g, n, t):
+            if (g, n) not in u_line:
+                u_line[g, n] = mix("u_line", [P, T, N])
+            nc.scalar.activation(u_line[g, n][:, t, :], v[g, n][:, t, :], ACT.Copy, scale=half_p[:, n, t:t + 1])
 
-        u_lin = {}
+        def lay_u(g, n):
+            u_mix[g, n] = mix("u_mix", [P, N, T])
+            nc.vector.tensor_copy(u_mix[g, n][:].rearrange("p (c i) t -> p c t i", i=4),
+                                  u_line[g, n][:].rearrange("p t (c i) -> p c t i", i=4))
 
-        def ul(g, ng, tn):
-            if (g, ng) not in u_lin:
-                u_lin[g, ng] = mix("u_lin", [P, T, N])
-            nc.scalar.activation(u_lin[g, ng][:, tn, :], v[g, ng][:, tn, :], ACT.Copy, scale=ph_f32[:, ng, tn:tn + 1])
+        def quantise_u(g, n):
+            quantise(u_codes[g, n], u_scales[g, n], u_mix[g, n][:].rearrange("p c t -> p (c t)"))
 
-        def ui(g, ng):
-            u_mix[g, ng] = mix("u_mix", [P, N, T])
-            nc.vector.tensor_copy(u_mix[g, ng][:], u_lin[g, ng][:].rearrange("p t k -> p k t"))
+        def drive_2(g, n, t):
+            drive(("z2", g, n, t), g, n, t, u_codes, u_scales)
 
-        def uq(g, ng):
-            quant(u_codes[g, ng][:], u_scales[g, ng][:], u_mix[g, ng][:].rearrange("p k t -> p (k t)"))
+        def tanh_2(g, n, t):
+            if (g, n) not in t2:
+                t2[g, n] = page("t2", [P, T, N], F32)
+            nc.scalar.activation(t2[g, n][:, t, :], banks["z2", g, n, t][:], ACT.Tanh, bias=b_col[:, n, t:t + 1])
 
-        def vs(g, ng):
-            nc.scalar.mul(v[g, ng][:], v[g, ng][:], 0.75)
+        def weigh(g, n):
+            nc.scalar.mul(v[g, n][:], v[g, n][:], 0.75)
 
-        def zc(g, ng, tn, half, parts):
-            n = N // parts
-            ps = bank["z", g, ng, tn, half] = psum.tile([P, N], F32, name="z", tag="bank", bufs=8)
-            drive_x(ps[:, 0:n], g, ng, tn, n * half, n * (half + 1))
+        def add(g, n, t):
+            nc.vector.scalar_tensor_tensor(out=t2[g, n][:, t, :], in0=v[g, n][:, t, :], scalar=0.75, in1=t2[g, n][:, t, :],
+                                           op0=ALU.mult, op1=ALU.add)
 
-        def z(g, ng, tn, half, parts):
-            n = N // parts
-            drive_a(bank["z", g, ng, tn, half][:, 0:n], g, ng, tn, u_codes, u_scales, n * half, n * (half + 1))
-
-        def Z(g, ng, tn, half, parts):
-            if (g, ng) not in e:
-                e[g, ng] = page("e", [P, T, N], F32)
-            n = N // parts
-            nc.scalar.activation(e[g, ng][:, tn, n * half:n * (half + 1)], bank["z", g, ng, tn, half][:, 0:n], ACT.Tanh, bias=b_col[:, ng, tn:tn + 1])
-
-        def cb(g, ng, tn, half, parts):
-            n = N // parts
-            k = slice(n * half, n * (half + 1))
-            nc.vector.scalar_tensor_tensor(out=e[g, ng][:, tn, k], in0=v[g, ng][:, tn, k], scalar=0.75, in1=e[g, ng][:, tn, k], op0=ALU.mult, op1=ALU.add)
-
-        def ga(g, ng, tn, half, parts):
-            n = N // parts
-            k = slice(n * half, n * (half + 1))
-            nc.gpsimd.tensor_tensor(out=e[g, ng][:, tn, k], in0=e[g, ng][:, tn, k], in1=v[g, ng][:, tn, k], op=ALU.add)
-
-        def o(g, ng, j):
-            ps = bank["o", g, ng, j] = psum.tile([P, T, P], F32, name="o", tag="bank", bufs=8)
-            c = slice(P * j, P * (j + 1))
-            for tn in range(T):
-                if (g, ng) in ACC:
-                    nc.tensor.matmul(ps[:, tn, :], v[g, ng][:, tn, c], ident[:], start=True, stop=False, is_transpose=True)
-                    nc.tensor.matmul(ps[:, tn, :], e[g, ng][:, tn, c], ident[:], start=False, stop=True, is_transpose=True)
+        def turn_out(g, n, j):
+            dst = banks["out", g, n, j] = bank([P, T, P])
+            tokens = slice(P * j, P * (j + 1))
+            for t in range(T):
+                if (g, n) == SUM_ON_TENSOR:
+                    nc.tensor.matmul(dst[:, t, :], v[g, n][:, t, tokens], ident[:], start=True, stop=False, is_transpose=True)
+                    nc.tensor.matmul(dst[:, t, :], t2[g, n][:, t, tokens], ident[:], start=False, stop=True, is_transpose=True)
                 else:
-                    nc.tensor.transpose(ps[:, tn, :], e[g, ng][:, tn, c], ident[:])
+                    nc.tensor.transpose(dst[:, t, :], t2[g, n][:, t, tokens], ident[:])
 
-        def F(g, ng, j):
-            if (g, ng) not in o_tile:
-                o_tile[g, ng] = page("o_tile", [P, T, N], F32)
+        def finish(g, n, j):
+            if (g, n) not in rows:
+                rows[g, n] = page("rows", [P, T, N], F32)
+            cols = slice(N * n, N * (n + 1))
             nc.vector.scalar_tensor_tensor(
-                out=o_tile[g, ng][:, j, :].rearrange("p (m t) -> p m t", t=T), in0=bank["o", g, ng, j][:].rearrange("p t m -> p m t"), scalar=0.25,
-                in1=h_nat[g][:, j, N * ng:N * (ng + 1)].rearrange("p (m t) -> p m t", t=T), op0=ALU.mult, op1=ALU.add)
+                out=rows[g, n][:, j, :].rearrange("p (m t) -> p m t", t=T),
+                in0=banks["out", g, n, j][:].rearrange("p t m -> p m t"), scalar=0.25,
+                in1=h_nat[g][:, j, cols].rearrange("p (m t) -> p m t", t=T), op0=ALU.mult, op1=ALU.add)
+            nc.sync.dma_start(out=out_rows[g, :, j, cols], in_=rows[g, n][:, j, :])
 
-        def st(g, ng, lo, hi):
-            nc.sync.dma_start(out=out_rows[g, :, lo:hi, N * ng:N * (ng + 1)], in_=o_tile[g, ng][:, lo:hi, :])
+        step = dict(
+            warm=warm, turn_w=turn_w, copy_w=copy_w, build_a=build_a, copy_a=copy_a, quantise_a=quantise_a, turn_h=turn_h,
+            copy_h=copy_h, gain_h=gain_h, quantise_h=quantise_h, halve_h=halve_h, widen_x=widen_x, turn_x=turn_x,
+            scale_x=scale_x, quantise_x=quantise_x, lay_win=lay_win, quantise_win=quantise_win, drive_1=drive_1,
+            tanh_1=tanh_1, state=state, gain_u=gain_u, lay_u=lay_u, quantise_u=quantise_u, drive_2=drive_2, tanh_2=tanh_2,
+            weigh=weigh, add=add, turn_out=turn_out, finish=finish)
 
-        step = dict(w=w, W=W, a=a, A=A, aq=aq, h_=h_, H_=H_, hg=hg, hq=hq, hh=hh, xc=xc, x_=x_, X_=X_, xq=xq, wl=wl, wq=wq,
-                    dm=dm, s=s, S=S, us=us, ug=ug, ul=ul, ui=ui, uq=uq, vs=vs, zc=zc, z=z, Z=Z, cb=cb, ga=ga, o=o, F=F, st=st)
-        for line in PLAN:
-            step[line[0]](*line[1:])
+        def needs(name, key):
+            g, n, t = (key + (0, 0, 0))[:3]
+            quad = range(T)
+            pair = range(2)
+            if name == "copy_w":
+                return [("turn_w",) + key]
+            if name == "build_a":
+                return [("copy_w", n, g, u) for u in pair]
+            if name == "copy_a":
+                return [("build_a",) + key]
+            if name == "quantise_a":
+                return [("copy_a",) + key + (q,) for q in quad]
+            if name == "copy_h":
+                return [("turn_h",) + key]
+            if name == "gain_h":
+                return [("copy_h", g, i, n) for i in pair]
+            if name == "quantise_h":
+                return [("gain_h",) + key]
+            if name == "halve_h":
+                return [("turn_h", g, i, k) for i in pair for k in pair]
+            if name == "turn_x":
+                return [("widen_x", g)]
+            if name == "scale_x":
+                return [("turn_x",) + key]
+            if name == "quantise_x":
+                return [("scale_x", g, i) for i in pair]
+            if name == "quantise_win":
+                return [("lay_win",) + key]
+            if name == "drive_1":
+                return ([("quantise_win", n), ("quantise_x", g)] + [("quantise_a", k, n) for k in pair]
+                        + [("quantise_h", g, k) for k in pair])
+            if name == "tanh_1":
+                return [("drive_1",) + key]
+            if name == "state":
+                return [("tanh_1", g, n, 2 * t + i) for i in pair]
+            if name == "gain_u":
+                return [("state", g, n, t // 2)]
+            if name in ("lay_u", "weigh"):
+                return [("gain_u", g, n, i) for i in quad]
+            if name == "quantise_u":
+                return [("lay_u",) + key]
+            if name == "drive_2":
+                return [("quantise_u", g, k) for k in pair]
+            if name == "tanh_2":
+                return [("drive_2",) + key]
+            if name == "add":
+                return [("tanh_2",) + key]
+            if name == "turn_out":
+                if (g, n) == SUM_ON_TENSOR:
+                    return [("weigh", g, n)] + [("tanh_2", g, n, i) for i in quad]
+                return [("add", g, n, i) for i in quad]
+            if name == "finish":
+                return [("turn_out",) + key, ("halve_h", g)]
+            return []
 
+        def run(name, *key, last=range(T)):
+            return [(name,) + key + (i,) for i in last]
 
-PLAN = (
-    ("h_", 0, 1, 0),
-    ("h_", 0, 0, 0),
-    ("H_", "V", 0, 1, 0),
-    ("h_", 0, 0, 1),
-    ("H_", "S", 0, 0, 0),
-    ("h_", 0, 1, 1),
-    ("H_", "V", 0, 0, 1),
-    ("dm", 2),
-    ("H_", "S", 0, 1, 1),
-    ("hh", "V", 0),
-    ("w", 0, 1, 1),
-    ("hg", 0, 1),
-    ("w", 0, 1, 0),
-    ("w", 0, 0, 0),
-    ("W", "V", 0, 1, 1),
-    ("W", "S", 0, 1, 0),
-    ("hq", 0, 1),
-    ("W", "S", 0, 0, 0),
-    ("a", 1, 0, 2),
-    ("hg", 0, 0),
-    ("xc", "S", 0),
-    ("w", 1, 0, 0),
-    ("w", 1, 0, 1),
-    ("W", "V", 1, 0, 0),
-    ("w", 1, 1, 0),
-    ("hq", 0, 0),
-    ("a", 1, 0, 1),
-    ("W", "S", 1, 0, 1),
-    ("wl", "V", 0),
-    ("a", 1, 0, 0),
-    ("W", "S", 1, 1, 0),
-    ("w", 1, 1, 1),
-    ("A", "S", 1, 0, 0),
-    ("xc", "V", 1),
-    ("x_", 0, 0),
-    ("W", "S", 1, 1, 1),
-    ("w", 0, 0, 1),
-    ("A", "S", 1, 0, 1),
-    ("X_", 0, 0),
-    ("a", 1, 0, 3),
-    ("W", "S", 0, 0, 1),
-    ("x_", 0, 1),
-    ("A", "S", 1, 0, 2),
-    ("wq", 0),
-    ("h_", 1, 1, 0),
-    ("A", "S", 1, 0, 3),
-    ("X_", 0, 1),
-    ("h_", 1, 1, 1),
-    ("H_", "S", 1, 1, 0),
-    ("a", 0, 0, 1),
-    ("H_", "S", 1, 1, 1),
-    ("aq", 1, 0),
-    ("a", 0, 0, 2),
-    ("wl", "S", 1),
-    ("xq", 0),
-    ("a", 0, 1, 0),
-    ("hg", 1, 1),
-    ("a", 0, 0, 0),
-    ("a", 1, 1, 0),
-    ("A", "V", 0, 0, 0),
-    ("a", 1, 1, 2),
-    ("A", "V", 1, 1, 0),
-    ("A", "S", 0, 0, 1),
-    ("a", 1, 1, 3),
-    ("wq", 1),
-    ("A", "S", 0, 0, 2),
-    ("a", 1, 1, 1),
-    ("hq", 1, 1),
-    ("A", "S", 0, 1, 0),
-    ("a", 0, 0, 3),
-    ("A", "V", 1, 1, 1),
-    ("h_", 1, 0, 0),
-    ("A", "S", 0, 0, 3),
-    ("x_", 1, 0),
-    ("A", "S", 1, 1, 2),
-    ("aq", 0, 0),
-    ("x_", 1, 1),
-    ("A", "S", 1, 1, 3),
-    ("X_", 1, 0),
-    ("s", 0, 0, 0),
-    ("H_", "S", 1, 0, 0),
-    ("aq", 1, 1),
-    ("s", 0, 0, 1),
-    ("S", 0, 0, 0),
-    ("X_", 1, 1),
-    ("a", 0, 1, 1),
-    ("S", 0, 0, 1),
-    ("a", 0, 1, 2),
-    ("A", "S", 0, 1, 1),
-    ("us", 0, 0, 0),
-    ("a", 0, 1, 3),
-    ("A", "S", 0, 1, 2),
-    ("h_", 1, 0, 1),
-    ("A", "S", 0, 1, 3),
-    ("xq", 1),
-    ("s", 0, 0, 3),
-    ("ul", 0, 0, 1),
-    ("aq", 0, 1),
-    ("ul", 0, 0, 0),
-    ("hh", "V", 1),
-    ("s", 0, 0, 2),
-    ("H_", "S", 1, 0, 1),
-    ("s", 0, 1, 2),
-    ("S", 0, 0, 2),
-    ("hg", 1, 0),
-    ("S", 0, 0, 3),
-    ("s", 0, 1, 3),
-    ("S", 0, 1, 2),
-    ("hq", 1, 0),
-    ("s", 0, 1, 1),
-    ("S", 0, 1, 3),
-    ("us", 0, 0, 1),
-    ("s", 0, 1, 0),
-    ("S", 0, 1, 1),
-    ("us", 0, 1, 1),
-    ("zc", 1, 0, 2, 0, 1),
-    ("S", 0, 1, 0),
-    ("zc", 0, 0, 1, 0, 1),
-    ("s", 1, 0, 3),
-    ("ul", 0, 0, 3),
-    ("us", 0, 1, 0),
-    ("ul", 0, 0, 2),
-    ("s", 1, 0, 2),
-    ("S", 1, 0, 3),
-    ("ui", 0, 0),
-    ("s", 1, 1, 2),
-    ("vs", 0, 0),
-    ("s", 1, 0, 1),
-    ("ug", 0, 1),
-    ("s", 1, 1, 1),
-    ("S", 1, 0, 1),
-    ("zc", 0, 1, 3, 0, 1),
-    ("zc", 0, 0, 2, 0, 1),
-    ("S", 1, 0, 2),
-    ("s", 1, 1, 0),
-    ("S", 1, 1, 1),
-    ("s", 1, 1, 3),
-    ("S", 1, 1, 0),
-    ("us", 1, 0, 1),
-    ("vs", 0, 1),
-    ("zc", 0, 0, 0, 0, 1),
-    ("s", 1, 0, 0),
-    ("uq", 0, 0),
-    ("us", 1, 1, 0),
-    ("S", 1, 0, 0),
-    ("uq", 0, 1),
-    ("S", 1, 1, 2),
-    ("zc", 0, 1, 1, 0, 1),
-    ("us", 1, 0, 0),
-    ("z", 0, 0, 0, 0, 1),
-    ("S", 1, 1, 3),
-    ("zc", 0, 0, 3, 0, 1),
-    ("Z", 0, 0, 0, 0, 1),
-    ("z", 0, 0, 3, 0, 1),
-    ("us", 1, 1, 1),
-    ("z", 0, 1, 1, 0, 1),
-    ("Z", 0, 0, 3, 0, 1),
-    ("z", 0, 0, 1, 0, 1),
-    ("ug", 1, 0),
-    ("Z", 0, 1, 1, 0, 1),
-    ("z", 0, 0, 2, 0, 1),
-    ("Z", 0, 0, 1, 0, 1),
-    ("ga", 0, 1, 1, 0, 1),
-    ("zc", 1, 1, 0, 1, 2),
-    ("Z", 0, 0, 2, 0, 1),
-    ("zc", 0, 1, 2, 0, 1),
-    ("z", 0, 1, 2, 0, 1),
-    ("z", 0, 1, 3, 0, 1),
-    ("Z", 0, 1, 2, 0, 1),
-    ("zc", 0, 1, 0, 0, 1),
-    ("Z", 0, 1, 3, 0, 1),
-    ("ug", 1, 1),
-    ("zc", 1, 1, 0, 0, 2),
-    ("ga", 0, 1, 2, 0, 1),
-    ("o", 0, 0, 3),
-    ("vs", 1, 0),
-    ("o", 0, 0, 1),
-    ("ga", 0, 1, 3, 0, 1),
-    ("z", 0, 1, 0, 0, 1),
-    ("zc", 1, 0, 1, 0, 1),
-    ("o", 0, 0, 0),
-    ("Z", 0, 1, 0, 0, 1),
-    ("uq", 1, 0),
-    ("ga", 0, 1, 0, 0, 1),
-    ("zc", 1, 0, 0, 0, 1),
-    ("uq", 1, 1),
-    ("F", 0, 0, 3),
-    ("z", 1, 0, 1, 0, 1),
-    ("F", 0, 0, 0),
-    ("z", 1, 0, 0, 0, 1),
-    ("st", 0, 0, 3, 4),
-    ("Z", 1, 0, 1, 0, 1),
-    ("F", 0, 0, 1),
-    ("zc", 1, 1, 2, 0, 2),
-    ("st", 0, 0, 0, 1),
-    ("zc", 1, 1, 1, 0, 2),
-    ("Z", 1, 0, 0, 0, 1),
-    ("z", 1, 1, 1, 0, 2),
-    ("ga", 1, 0, 1, 0, 1),
-    ("zc", 1, 1, 2, 1, 2),
-    ("st", 0, 0, 1, 2),
-    ("zc", 1, 1, 3, 0, 2),
-    ("Z", 1, 1, 1, 0, 2),
-    ("z", 1, 1, 2, 0, 2),
-    ("z", 1, 1, 0, 0, 2),
-    ("cb", 1, 1, 1, 0, 2),
-    ("Z", 1, 1, 2, 0, 2),
-    ("z", 1, 1, 3, 0, 2),
-    ("ga", 1, 0, 0, 0, 1),
-    ("Z", 1, 1, 0, 0, 2),
-    ("zc", 1, 1, 3, 1, 2),
-    ("cb", 1, 1, 2, 0, 2),
-    ("z", 1, 1, 2, 1, 2),
-    ("Z", 1, 1, 3, 0, 2),
-    ("cb", 1, 1, 0, 0, 2),
-    ("zc", 1, 1, 1, 1, 2),
-    ("Z", 1, 1, 2, 1, 2),
-    ("z", 1, 1, 0, 1, 2),
-    ("cb", 1, 1, 3, 0, 2),
-    ("z", 1, 1, 1, 1, 2),
-    ("Z", 1, 1, 0, 1, 2),
-    ("cb", 1, 1, 2, 1, 2),
-    ("o", 0, 1, 0),
-    ("Z", 1, 1, 1, 1, 2),
-    ("cb", 1, 1, 0, 1, 2),
-    ("o", 0, 1, 3),
-    ("F", 0, 1, 0),
-    ("o", 0, 1, 1),
-    ("o", 1, 1, 1),
-    ("F", 0, 1, 3),
-    ("st", 0, 1, 0, 1),
-    ("o", 0, 1, 2),
-    ("z", 1, 0, 2, 0, 1),
-    ("F", 0, 1, 1),
-    ("st", 0, 1, 3, 4),
-    ("zc", 1, 0, 3, 0, 1),
-    ("F", 0, 1, 2),
-    ("Z", 1, 0, 2, 0, 1),
-    ("st", 0, 1, 1, 2),
-    ("z", 1, 1, 3, 1, 2),
-    ("z", 1, 0, 3, 0, 1),
-    ("F", 1, 1, 1),
-    ("Z", 1, 1, 3, 1, 2),
-    ("st", 0, 1, 2, 3),
-    ("ga", 1, 0, 2, 0, 1),
-    ("o", 1, 1, 0),
-    ("cb", 1, 1, 3, 1, 2),
-    ("Z", 1, 0, 3, 0, 1),
-    ("st", 1, 1, 1, 2),
-    ("cb", 1, 1, 1, 1, 2),
-    ("F", 1, 1, 0),
-    ("ga", 1, 0, 3, 0, 1),
-    ("o", 1, 1, 3),
-    ("o", 1, 1, 2),
-    ("F", 1, 1, 3),
-    ("st", 1, 1, 0, 1),
-    ("o", 0, 0, 2),
-    ("F", 1, 1, 2),
-    ("st", 1, 1, 3, 4),
-    ("o", 1, 0, 3),
-    ("F", 0, 0, 2),
-    ("st", 1, 1, 2, 3),
-    ("o", 1, 0, 1),
-    ("F", 1, 0, 3),
-    ("st", 0, 0, 2, 3),
-    ("o", 1, 0, 2),
-    ("F", 1, 0, 1),
-    ("st", 1, 0, 3, 4),
-    ("o", 1, 0, 0),
-    ("F", 1, 0, 2),
-    ("st", 1, 0, 1, 2),
-    ("F", 1, 0, 0),
-    ("st", 1, 0, 2, 3),
-    ("st", 1, 0, 0, 1),
-)
+        def one(name, *key):
+            return [(name,) + key]
+
+        two = range(2)
+        tensor = (
+            one("warm", 7) + run("turn_h", 0, 0, last=two) + run("turn_h", 0, 1, last=two) + one("warm", 2)
+            + run("turn_w", 0, 0, last=two) + run("turn_w", 0, 1, last=two)
+            + run("build_a", 0, 0, last=[0]) + run("turn_w", 1, 0, last=[0]) + run("build_a", 0, 0, last=[1])
+            + run("turn_w", 1, 0, last=[1]) + run("turn_w", 1, 1, last=two) + run("build_a", 0, 0, last=[2, 3])
+            + run("turn_x", 0, last=two) + run("turn_h", 1, 0, last=[0]) + run("build_a", 1, 0)
+            + run("turn_h", 1, 0, last=[1]) + run("turn_h", 1, 1, last=two) + run("build_a", 1, 1)
+            + run("drive_1", 0, 0) + run("build_a", 0, 1) + run("turn_x", 1, last=two)
+            + run("drive_1", 0, 1) + run("drive_1", 1, 0) + run("drive_1", 1, 1)
+            + run("drive_2", 0, 0) + run("drive_2", 0, 1) + run("drive_2", 1, 1, last=[0, 1, 2]) + run("turn_out", 0, 0)
+            + run("drive_2", 1, 1, last=[3]) + run("turn_out", 0, 1) + run("drive_2", 1, 0)
+            + run("turn_out", 1, 1) + run("turn_out", 1, 0)
+        )
+        vector = (
+            one("copy_h", 0, 0, 0) + one("halve_h", 0) + one("gain_h", 0, 1) + one("gain_h", 0, 0) + one("quantise_h", 0, 0)
+            + one("copy_w", 0, 1, 0) + one("quantise_h", 0, 1)
+            + one("lay_win", 1) + one("quantise_win", 1) + one("widen_x", 1) + one("lay_win", 0) + one("quantise_win", 0)
+            + one("quantise_a", 0, 0) + run("scale_x", 0, last=two) + one("quantise_x", 0) + one("quantise_a", 1, 0)
+            + one("gain_h", 1, 0) + one("quantise_h", 1, 0) + one("halve_h", 1) + one("gain_h", 1, 1) + one("quantise_h", 1, 1)
+            + one("quantise_a", 1, 1) + run("state", 0, 0, last=two)
+            + one("quantise_a", 0, 1) + run("scale_x", 1, last=two) + one("quantise_x", 1)
+            + one("state", 0, 1, 0) + one("lay_u", 0, 0) + one("state", 0, 1, 1) + run("state", 1, 0, last=two)
+            + one("lay_u", 0, 1) + one("quantise_u", 0, 0) + one("quantise_u", 0, 1) + run("state", 1, 1, last=two)
+            + one("lay_u", 1, 0) + one("quantise_u", 1, 0) + one("lay_u", 1, 1)
+            + one("add", 0, 0, 0) + one("quantise_u", 1, 1) + run("add", 0, 0, last=[1, 2, 3]) + run("add", 0, 1)
+            + run("finish", 0, 0) + run("add", 1, 1) + run("finish", 0, 1) + run("finish", 1, 1) + run("finish", 1, 0)
+        )
+        scalar = (
+            one("copy_h", 0, 0, 1) + run("copy_h", 0, 1, last=two) + run("copy_w", 0, 0, last=two) + one("copy_w", 0, 1, 1)
+            + one("widen_x", 0) + run("copy_w", 1, 0, last=two) + run("copy_w", 1, 1, last=two) + run("copy_a", 0, 0)
+            + one("copy_h", 1, 0, 0) + run("copy_a", 1, 0) + one("copy_h", 1, 0, 1) + run("copy_h", 1, 1, last=two)
+            + run("copy_a", 1, 1) + run("tanh_1", 0, 0) + run("copy_a", 0, 1) + run("gain_u", 0, 0)
+            + run("tanh_1", 0, 1) + run("gain_u", 0, 1, last=[0]) + run("tanh_1", 1, 0, last=two)
+            + run("gain_u", 0, 1, last=[1]) + run("tanh_1", 1, 0, last=[2, 3]) + run("gain_u", 0, 1, last=[2, 3])
+            + run("tanh_1", 1, 1) + run("gain_u", 1, 0) + run("gain_u", 1, 1)
+            + run("tanh_2", 0, 0) + run("tanh_2", 0, 1) + run("tanh_2", 1, 1) + one("weigh", 1, 0) + run("tanh_2", 1, 0)
+        )
+
+        copies = ((vector, nc.vector.tensor_copy), (scalar, nc.scalar.copy), (tensor, None))
+        place = [0, 0, 0]
+        issued = set()
+
+        def issue():
+            for i, (queue, copy) in enumerate(copies):
+                if place[i] < len(queue):
+                    name, key = queue[place[i]][0], queue[place[i]][1:]
+                    if all(need in issued for need in needs(name, key)):
+                        if name in ("copy_w", "copy_a", "copy_h", "widen_x", "lay_win"):
+                            step[name](copy, *key)
+                        else:
+                            step[name](*key)
+                        issued.add(queue[place[i]])
+                        place[i] += 1
+                        return True
+            return False
+
+        for i in range(len(tensor) + len(vector) + len(scalar)):
+            assert issue(), "a queue waits for a step that no queue holds"

@@ -217,7 +217,8 @@ def tile_antisymmetricssprk2step_kernel(tc, h, x_bytes, x_scale, w, win, b, p, r
 
         def lay_win(copy, n):
             win_mix[n] = mix("win_mix", [P, T, P, T])
-            copy(win_mix[n][:], win_nat[:, :, N * n:N * (n + 1)].rearrange("p t (m i) -> p i m t", i=T))
+            copy(win_mix[n][:].rearrange("p i m t -> p m t i"),
+                 win_nat[:, :, N * n:N * (n + 1)].rearrange("p t (m i) -> p m t i", i=T))
 
         def quantise_win(n):
             quantise(win_codes[n], win_scales[n], win_mix[n][:].rearrange("p i m t -> p (i m t)"))

from contextlib import ExitStack

import concourse.mybir as mybir
from concourse.masks import make_identity

F32 = mybir.dt.float32
BF16 = mybir.dt.bfloat16
U32 = mybir.dt.uint32
U8 = mybir.dt.uint8
FP8 = mybir.dt.float8_e4m3fn
FP8X4 = mybir.dt.float8_e4m3fn_x4
ALU = mybir.AluOpType
ACT = mybir.ActivationFunctionType

B, D, X = 1024, 1024, 512
P = 128
T = 4
N = P * T
HALVES = B // N
GROUPS = D // N

BANKS = 8
PAGES = 7
MIXES = 12

SUM_ON_TENSOR = (1, 0)

FLOPS = 2 * B * D * (X + 2 * D)


def tile_antisymmetricssprk2step_kernel(tc, h, x_bytes, x_scale, w, win, b, p, r, out):
    nc = tc.nc
    with ExitStack() as ctx:
        keep = ctx.enter_context(tc.tile_pool(name="keep", bufs=1))
        work = ctx.enter_context(tc.tile_pool(name="work", bufs=1))
        psum = ctx.enter_context(tc.psum_pool(name="psum", bufs=BANKS))
        ctx.enter_context(tc.manual_schedule())

        def kept(name, shape, dtype):
            return keep.tile(shape, dtype, name=name, align_bytes=64)

        def kept_grid(name, shape, dtype):
            return {(i, j): kept("%s_%d%d" % (name, i, j), shape, dtype) for i in range(2) for j in range(2)}

        def page(name, shape, dtype):
            return work.tile(shape, dtype, name=name, tag="page", bufs=PAGES, align_bytes=64)

        def mix(name, shape):
            return work.tile(shape, BF16, name=name, tag="mix", bufs=MIXES, align_bytes=64)

        def bank(shape):
            return psum.tile(shape, F32, name="bank")

        h_rows = h.rearrange("(g p t) c -> g p t c", p=P, t=T)
        w_rows = w.rearrange("(g p t) c -> g p t c", p=P, t=T)
        x_rows = x_bytes.rearrange("(g p t) c -> g p t c", p=P, t=T)
        out_rows = out.rearrange("(g p t) c -> g p t c", p=P, t=T)
        h_nat = [kept("h_nat_%d" % g, [P, T, D], BF16) for g in range(HALVES)]
        w_nat = [page("w_nat_%d" % g, [P, T, D], BF16) for g in range(GROUPS)]
        win_nat = page("win_nat", [P, T, D], BF16)
        x_raw = [kept("x_raw_%d" % g, [P, T, X], U8) for g in range(HALVES)]

        r_col = kept("r_col", [P, GROUPS, T], BF16)
        p_col = kept("p_col", [P, GROUPS, T], BF16)
        b_col = kept("b_col", [P, GROUPS, T], BF16)
        s_col = kept("s_col", [P, T], F32)
        for col, vec in ((r_col, r), (p_col, p), (b_col, b)):
            nc.scalar.dma_start(out=col[:], in_=vec.rearrange("(g p t) -> p g t", p=P, t=T))
        nc.scalar.dma_start(out=s_col[:], in_=x_scale.rearrange("o (p t) -> p (o t)", p=P, t=T))

        for lo, hi in ((0, 1), (1, 2), (2, 4)):
            nc.sync.dma_start(out=h_nat[0][:, lo:hi, :], in_=h_rows[0, :, lo:hi, :])
        for g in range(GROUPS):
            nc.sync.dma_start(out=w_nat[g][:], in_=w_rows[g])
        nc.sync.dma_start(out=x_raw[0][:], in_=x_rows[0])
        nc.sync.dma_start(out=win_nat[:], in_=win.rearrange("(p t) c -> p t c", p=P, t=T))
        nc.sync.dma_start(out=x_raw[1][:], in_=x_rows[1])
        nc.sync.dma_start(out=h_nat[1][:], in_=h_rows[1])

        a_codes = kept_grid("a_codes", [P, N], U32)
        a_scales = kept_grid("a_scales", [P, N], U8)
        hp_codes = kept_grid("hp_codes", [P, N], U32)
        hp_scales = kept_grid("hp_scales", [P, N], U8)
        u_codes = kept_grid("u_codes", [P, N], U32)
        u_scales = kept_grid("u_scales", [P, N], U8)
        x_codes = [kept("x_codes_%d" % g, [P, N], U32) for g in range(HALVES)]
        x_scales = [kept("x_scales_%d" % g, [P, N], U8) for g in range(HALVES)]
        win_codes = [kept("win_codes_%d" % g, [P, N], U32) for g in range(GROUPS)]
        win_scales = [kept("win_scales_%d" % g, [P, N], U8) for g in range(GROUPS)]
        x_val = [kept("x_val_%d" % g, [P, T, X], BF16) for g in range(HALVES)]
        h_turned = kept_grid("h_turned", [P, N, T], BF16)
        v = kept_grid("v", [P, T, N], F32)
        w_turned, a_mix, hp_mix, x_mix, win_mix, u_line, u_mix, t2, rows, banks = ({} for i in range(10))

        zero_codes, zero_scales = u_codes[1, 1], u_scales[1, 1]
        nc.vector.memset(zero_codes[:], 0)
        nc.vector.memset(zero_scales[:].bitcast(U32), 0)
        ident = kept("ident", [P, P], F32)
        make_identity(nc, ident[:])
        table = kept("table", [P, 1], F32)
        nc.vector.memset(table[:], 0.0)
        nc.scalar.activation(table[:], table[:], ACT.Tanh)
        ident_bf = kept("ident_bf", [P, P], BF16)
        nc.vector.tensor_copy(ident_bf[:], ident[:])
        diag = kept("diag", [P, GROUPS * T, P], BF16)
        minus = kept("minus", [P, GROUPS * T, P], BF16)
        nc.vector.tensor_tensor(
            out=diag[:],
            in0=ident_bf[:].unsqueeze(1).to_broadcast([P, GROUPS * T, P]),
            in1=r_col[:].rearrange("p g t -> p (g t)").unsqueeze(2).to_broadcast([P, GROUPS * T, P]),
            op=ALU.mult,
        )
        nc.vector.tensor_scalar(out=minus[:], in0=diag[:], scalar1=-1.0, scalar2=None, op0=ALU.mult)
        half_p = kept("half_p", [P, GROUPS, T], F32)
        nc.vector.tensor_scalar(out=half_p[:], in0=p_col[:], scalar1=0.5, scalar2=None, op0=ALU.mult)

        def quantise(codes, scales, in_):
            nc.vector.quantize_mx(out=codes[:].bitcast(FP8X4), scales=scales[:], in_=in_)

        def words(tile, t):
            return tile[:, t, :].bitcast(F32)

        def turn(dst, tile, t, contraction_pass, u):
            first = contraction_pass * N // 2
            nc.tensor.transpose(dst, words(tile, t)[:, first + u:first + N // 2:2], ident[:])

        def multiply(dst, lhs, lhs_scale, cols, rhs, rhs_scale, start, stop):
            nc.tensor.matmul_mx(
                dst, lhsT=lhs[:, cols].bitcast(FP8X4), lhsT_scale=lhs_scale[:, cols],
                rhs=rhs[:].bitcast(FP8X4), rhs_scale=rhs_scale[:], start=start, stop=stop)

        def drive(key, half, group, t, codes, scales):
            acc = banks[key] = bank([P, N])
            cols = slice(P * t, P * (t + 1))
            multiply(acc[:], win_codes[group], win_scales[group], cols, x_codes[half], x_scales[half], True, False)
            for k in range(GROUPS):
                multiply(acc[:], a_codes[k, group], a_scales[k, group], cols, codes[half, k], scales[half, k],
                         False, k == GROUPS - 1)

        def warm(passes):
            dst = bank([P, N])
            for i in range(passes):
                multiply(dst[:], zero_codes, zero_scales, slice(0, P), zero_codes, zero_scales, True, True)

        def turn_w(n, k, u):
            dst = banks["w", n, k, u] = bank([P, T, P])
            for t in range(T):
                turn(dst[:, t, :], w_nat[n], t, k, u)

        def copy_w(copy, n, k, u):
            if (k, n) not in w_turned:
                w_turned[k, n] = mix("w_turned", [P, 2, N, 2])
            dst = w_turned[k, n][:, u, :, :].rearrange("p n e -> p (n e)").bitcast(F32)
            copy(dst.rearrange("p (m t) -> p m t", t=T), banks["w", n, k, u][:].rearrange("p t m -> p m t"))

        def build_a(k, n, q):
            acc = banks["a", k, n, q] = bank([P, T, P])
            cols = slice(P * q, P * (q + 1))
            for t in range(T):
                nc.tensor.matmul(acc[:, t, :], diag[:, k * T + t, :], w_nat[k][:, t, N * n + P * q:N * n + P * (q + 1)],
                                 start=True, stop=False)
                nc.tensor.matmul(acc[:, t, :], minus[:, k * T + t, :], w_turned[k, n][:, t // 2, cols, t % 2],
                                 start=False, stop=True)

        def copy_a(copy, k, n, q):
            if (k, n) not in a_mix:
                a_mix[k, n] = mix("a_mix", [P, T, P, T])
            m = P // T
            copy(a_mix[k, n][:, :, m * q:m * (q + 1), :], banks["a", k, n, q][:].rearrange("p t (m i) -> p i m t", i=T))

        def quantise_a(k, n):
            quantise(a_codes[k, n], a_scales[k, n], a_mix[k, n][:].rearrange("p i m t -> p (i m t)"))

        def turn_h(g, pair, k):
            dst = banks["h", g, pair, k] = bank([P, 2, 2, P])
            for j in range(2):
                for u in range(2):
                    turn(dst[:, u, j, :], h_nat[g], 2 * pair + j, k, u)

        def copy_h(copy, g, pair, k):
            dst = h_turned[g, k][:, 2 * P * pair:2 * P * (pair + 1), :].rearrange("p c t -> p (c t)").bitcast(F32)
            copy(dst.rearrange("p (c u) -> p c u", u=2), banks["h", g, pair, k][:].rearrange("p u j i -> p (j i) u"))

        def gain_h(g, k):
            hp_mix[g, k] = mix("hp_mix", [P, N, T])
            nc.vector.tensor_tensor(out=hp_mix[g, k][:], in0=h_turned[g, k][:],
                                    in1=p_col[:, k, :].unsqueeze(1).to_broadcast([P, N, T]), op=ALU.mult)

        def quantise_h(g, k):
            quantise(hp_codes[g, k], hp_scales[g, k], hp_mix[g, k][:].rearrange("p c t -> p (c t)"))

        def halve_h(g):
            nc.vector.tensor_scalar(out=h_nat[g][:], in0=h_nat[g][:], scalar1=0.5, scalar2=None, op0=ALU.mult)

        def widen_x(copy, g):
            copy(x_val[g][:], x_raw[g][:].bitcast(FP8))

        def turn_x(g, pair):
            dst = banks["x", g, pair] = bank([P, 2, 2, P])
            for j in range(2):
                for u in range(2):
                    turn(dst[:, u, j, :], x_val[g], 2 * pair + j, 0, u)

        def scale_x(g, pair):
            if g not in x_mix:
                x_mix[g] = mix("x_mix", [P, N, T])
            turned = banks["x", g, pair][:].rearrange("p u j i -> p u (j i)").bitcast(BF16)
            nc.vector.tensor_tensor(
                out=x_mix[g][:, 2 * P * pair:2 * P * (pair + 1), :].rearrange("p c (u e) -> p c u e", e=2),
                in0=turned.rearrange("p u (c e) -> p c u e", e=2),
                in1=s_col[:].rearrange("p (u e) -> p u e", e=2).unsqueeze(1).to_broadcast([P, 2 * P, 2, 2]),
                op=ALU.mult,
            )

        def quantise_x(g):
            quantise(x_codes[g], x_scales[g], x_mix[g][:].rearrange("p c t -> p (c t)"))

        def lay_win(copy, n):
            win_mix[n] = mix("win_mix", [P, T, P, T])
            copy(win_mix[n][:].rearrange("p i m t -> p m t i"),
                 win_nat[:, :, N * n:N * (n + 1)].rearrange("p t (m i) -> p m t i", i=T))

        def quantise_win(n):
            quantise(win_codes[n], win_scales[n], win_mix[n][:].rearrange("p i m t -> p (i m t)"))

        def drive_1(g, n, t):
            drive(("z1", g, n, t), g, n, t, hp_codes, hp_scales)

        def tanh_1(g, n, t):
            nc.scalar.activation(v[g, n][:, t, :], banks["z1", g, n, t][:], ACT.Tanh, bias=b_col[:, n, t:t + 1])

        def state(g, n, s):
            ts = slice(2 * s, 2 * s + 2)
            nc.vector.scalar_tensor_tensor(
                out=v[g, n][:, ts, :], in0=h_turned[g, n][:, :, ts].rearrange("p c t -> p t c"), scalar=1.5,
                in1=v[g, n][:, ts, :], op0=ALU.mult, op1=ALU.add)

        def gain_u(g, n, t):
            if (g, n) not in u_line:
                u_line[g, n] = mix("u_line", [P, T, N])
            nc.scalar.activation(u_line[g, n][:, t, :], v[g, n][:, t, :], ACT.Copy, scale=half_p[:, n, t:t + 1])

        def lay_u(g, n):
            u_mix[g, n] = mix("u_mix", [P, N, T])
            nc.vector.tensor_copy(u_mix[g, n][:].rearrange("p (c i) t -> p c t i", i=4),
                                  u_line[g, n][:].rearrange("p t (c i) -> p c t i", i=4))

        def quantise_u(g, n):
            quantise(u_codes[g, n], u_scales[g, n], u_mix[g, n][:].rearrange("p c t -> p (c t)"))

        def drive_2(g, n, t):
            drive(("z2", g, n, t), g, n, t, u_codes, u_scales)

        def tanh_2(g, n, t):
            if (g, n) not in t2:
                t2[g, n] = page("t2", [P, T, N], F32)
            nc.scalar.activation(t2[g, n][:, t, :], banks["z2", g, n, t][:], ACT.Tanh, bias=b_col[:, n, t:t + 1])

        def weigh(g, n):
            nc.scalar.mul(v[g, n][:], v[g, n][:], 0.75)

        def add(g, n, t):
            nc.vector.scalar_tensor_tensor(out=t2[g, n][:, t, :], in0=v[g, n][:, t, :], scalar=0.75, in1=t2[g, n][:, t, :],
                                           op0=ALU.mult, op1=ALU.add)

        def turn_out(g, n, j):
            dst = banks["out", g, n, j] = bank([P, T, P])
            tokens = slice(P * j, P * (j + 1))
            for t in range(T):
                if (g, n) == SUM_ON_TENSOR:
                    nc.tensor.matmul(dst[:, t, :], v[g, n][:, t, tokens], ident[:], start=True, stop=False, is_transpose=True)
                    nc.tensor.matmul(dst[:, t, :], t2[g, n][:, t, tokens], ident[:], start=False, stop=True, is_transpose=True)
                else:
                    nc.tensor.transpose(dst[:, t, :], t2[g, n][:, t, tokens], ident[:])

        def finish(g, n, j):
            if (g, n) not in rows:
                rows[g, n] = page("rows", [P, T, N], F32)
            cols = slice(N * n, N * (n + 1))
            nc.vector.scalar_tensor_tensor(
                out=rows[g, n][:, j, :].rearrange("p (m t) -> p m t", t=T),
                in0=banks["out", g, n, j][:].rearrange("p t m -> p m t"), scalar=0.25,
                in1=h_nat[g][:, j, cols].rearrange("p (m t) -> p m t", t=T), op0=ALU.mult, op1=ALU.add)
            nc.sync.dma_start(out=out_rows[g, :, j, cols], in_=rows[g, n][:, j, :])

        step = dict(
            warm=warm, turn_w=turn_w, copy_w=copy_w, build_a=build_a, copy_a=copy_a, quantise_a=quantise_a, turn_h=turn_h,
            copy_h=copy_h, gain_h=gain_h, quantise_h=quantise_h, halve_h=halve_h, widen_x=widen_x, turn_x=turn_x,
            scale_x=scale_x, quantise_x=quantise_x, lay_win=lay_win, quantise_win=quantise_win, drive_1=drive_1,
            tanh_1=tanh_1, state=state, gain_u=gain_u, lay_u=lay_u, quantise_u=quantise_u, drive_2=drive_2, tanh_2=tanh_2,
            weigh=weigh, add=add, turn_out=turn_out, finish=finish)

        def needs(name, key):
            g, n, t = (key + (0, 0, 0))[:3]
            quad = range(T)
            pair = range(2)
            if name == "copy_w":
                return [("turn_w",) + key]
            if name == "build_a":
                return [("copy_w", n, g, u) for u in pair]
            if name == "copy_a":
                return [("build_a",) + key]
            if name == "quantise_a":
                return [("copy_a",) + key + (q,) for q in quad]
            if name == "copy_h":
                return [("turn_h",) + key]
            if name == "gain_h":
                return [("copy_h", g, i, n) for i in pair]
            if name == "quantise_h":
                return [("gain_h",) + key]
            if name == "halve_h":
                return [("turn_h", g, i, k) for i in pair for k in pair]
            if name == "turn_x":
                return [("widen_x", g)]
            if name == "scale_x":
                return [("turn_x",) + key]
            if name == "quantise_x":
                return [("scale_x", g, i) for i in pair]
            if name == "quantise_win":
                return [("lay_win",) + key]
            if name == "drive_1":
                return ([("quantise_win", n), ("quantise_x", g)] + [("quantise_a", k, n) for k in pair]
                        + [("quantise_h", g, k) for k in pair])
            if name == "tanh_1":
                return [("drive_1",) + key]
            if name == "state":
                return [("tanh_1", g, n, 2 * t + i) for i in pair]
            if name == "gain_u":
                return [("state", g, n, t // 2)]
            if name in ("lay_u", "weigh"):
                return [("gain_u", g, n, i) for i in quad]
            if name == "quantise_u":
                return [("lay_u",) + key]
            if name == "drive_2":
                return [("quantise_u", g, k) for k in pair]
            if name == "tanh_2":
                return [("drive_2",) + key]
            if name == "add":
                return [("tanh_2",) + key]
            if name == "turn_out":
                if (g, n) == SUM_ON_TENSOR:
                    return [("weigh", g, n)] + [("tanh_2", g, n, i) for i in quad]
                return [("add", g, n, i) for i in quad]
            if name == "finish":
                return [("turn_out",) + key, ("halve_h", g)]
            return []

        def run(name, *key, last=range(T)):
            return [(name,) + key + (i,) for i in last]

        def one(name, *key):
            return [(name,) + key]

        two = range(2)
        tensor = (
            one("warm", 7) + run("turn_h", 0, 0, last=two) + run("turn_h", 0, 1, last=two) + one("warm", 2)
            + run("turn_w", 0, 0, last=two) + run("turn_w", 0, 1, last=two)
            + run("build_a", 0, 0, last=[0]) + run("turn_w", 1, 0, last=[0]) + run("build_a", 0, 0, last=[1])
            + run("turn_w", 1, 0, last=[1]) + run("turn_w", 1, 1, last=two) + run("build_a", 0, 0, last=[2, 3])
            + run("turn_x", 0, last=two) + run("turn_h", 1, 0, last=[0]) + run("build_a", 1, 0)
            + run("turn_h", 1, 0, last=[1]) + run("turn_h", 1, 1, last=two) + run("build_a", 1, 1)
            + run("drive_1", 0, 0) + run("build_a", 0, 1) + run("turn_x", 1, last=two)
            + run("drive_1", 0, 1) + run("drive_1", 1, 0) + run("drive_1", 1, 1)
            + run("drive_2", 0, 0) + run("drive_2", 0, 1) + run("drive_2", 1, 1, last=[0, 1, 2]) + run("turn_out", 0, 0)
            + run("drive_2", 1, 1, last=[3]) + run("turn_out", 0, 1) + run("drive_2", 1, 0)
            + run("turn_out", 1, 1) + run("turn_out", 1, 0)
        )
        vector = (
            one("copy_h", 0, 0, 0) + one("halve_h", 0) + one("gain_h", 0, 1) + one("gain_h", 0, 0) + one("quantise_h", 0, 0)
            + one("copy_w", 0, 1, 0) + one("quantise_h", 0, 1)
            + one("lay_win", 1) + one("quantise_win", 1) + one("widen_x", 1) + one("lay_win", 0) + one("quantise_win", 0)
            + one("quantise_a", 0, 0) + run("scale_x", 0, last=two) + one("quantise_x", 0) + one("quantise_a", 1, 0)
            + one("gain_h", 1, 0) + one("quantise_h", 1, 0) + one("halve_h", 1) + one("gain_h", 1, 1) + one("quantise_h", 1, 1)
            + one("quantise_a", 1, 1) + run("state", 0, 0, last=two)
            + one("quantise_a", 0, 1) + run("scale_x", 1, last=two) + one("quantise_x", 1)
            + one("state", 0, 1, 0) + one("lay_u", 0, 0) + one("state", 0, 1, 1) + run("state", 1, 0, last=two)
            + one("lay_u", 0, 1) + one("quantise_u", 0, 0) + one("quantise_u", 0, 1) + run("state", 1, 1, last=two)
            + one("lay_u", 1, 0) + one("quantise_u", 1, 0) + one("lay_u", 1, 1)
            + one("add", 0, 0, 0) + one("quantise_u", 1, 1) + run("add", 0, 0, last=[1, 2, 3]) + run("add", 0, 1)
            + run("finish", 0, 0) + run("add", 1, 1) + run("finish", 0, 1) + run("finish", 1, 1) + run("finish", 1, 0)
        )
        scalar = (
            one("copy_h", 0, 0, 1) + run("copy_h", 0, 1, last=two) + run("copy_w", 0, 0, last=two) + one("copy_w", 0, 1, 1)
            + one("widen_x", 0) + run("copy_w", 1, 0, last=two) + run("copy_w", 1, 1, last=two) + run("copy_a", 0, 0)
            + one("copy_h", 1, 0, 0) + run("copy_a", 1, 0) + one("copy_h", 1, 0, 1) + run("copy_h", 1, 1, last=two)
            + run("copy_a", 1, 1) + run("tanh_1", 0, 0) + run("copy_a", 0, 1) + run("gain_u", 0, 0)
            + run("tanh_1", 0, 1) + run("gain_u", 0, 1, last=[0]) + run("tanh_1", 1, 0, last=two)
            + run("gain_u", 0, 1, last=[1]) + run("tanh_1", 1, 0, last=[2, 3]) + run("gain_u", 0, 1, last=[2, 3])
            + run("tanh_1", 1, 1) + run("gain_u", 1, 0) + run("gain_u", 1, 1)
            + run("tanh_2", 0, 0) + run("tanh_2", 0, 1) + run("tanh_2", 1, 1) + one("weigh", 1, 0) + run("tanh_2", 1, 0)
        )

        copies = ((vector, nc.vector.tensor_copy), (scalar, nc.scalar.copy), (tensor, None))
        place = [0, 0, 0]
        issued = set()

        def issue():
            for i, (queue, copy) in enumerate(copies):
                if place[i] < len(queue):
                    name, key = queue[place[i]][0], queue[place[i]][1:]
                    if all(need in issued for need in needs(name, key)):
                        if name in ("copy_w", "copy_a", "copy_h", "widen_x", "lay_win"):
                            step[name](copy, *key)
                        else:
                            step[name](*key)
                        issued.add(queue[place[i]])
                        place[i] += 1
                        return True
            return False

        for i in range(len(tensor) + len(vector) + len(scalar)):
            assert issue(), "a queue waits for a step that no queue holds"
